import numpy as np
import ml_dtypes


def mxq(x, axis, fmt="e4m3"):
    dtype, down = {"e4m3": (ml_dtypes.float8_e4m3fn, 7), "e5m2": (ml_dtypes.float8_e5m2, 14)}[fmt]
    v = np.moveaxis(np.asarray(x, np.float32).astype(ml_dtypes.bfloat16).astype(np.float64), axis, -1)
    blocks = v.reshape(v.shape[:-1] + (-1, 32))
    amax = np.abs(blocks).max(-1, keepdims=True)
    byte = np.maximum(np.where(amax > 0, np.frexp(amax)[1] - 1 + 127, 0) - down, 1)
    scale = np.exp2(byte - 127.0)
    codes = (blocks / scale).astype(np.float32).astype(dtype).astype(np.float64)
    return np.moveaxis((codes * scale).reshape(v.shape), -1, axis)


WIDE = False


def mx_kscale(k):
    if not WIDE:
        return np.ones(k)
    levels = np.array([10, -10, 5, -5, 0])
    if k % 512:
        return np.exp2(np.random.permutation(np.resize(levels, k // 32))).repeat(32)
    a = np.empty((k // 512, 16))
    for p in range(k // 512):
        a[p, :8] = np.random.permutation(np.resize(levels, 8))
        for g in range(8):
            far = levels[np.abs(levels - a[p, g]) >= 10]
            a[p, g + 8] = far[np.random.randint(len(far))]
    return np.exp2(a.ravel()).repeat(32)


def f64(x):
    return np.asarray(x).astype(np.float64)


def striped(idx):
    return np.tile(idx.reshape(-1, 16).T, (8, 1)).astype(np.uint16)


def unstriped(offs):
    return offs[:16].T.reshape(-1).astype(np.int64)


E2M1 = np.array([0.0, 0.5, 1.0, 1.5, 2.0, 3.0, 4.0, 6.0, -0.0, -0.5, -1.0, -1.5, -2.0, -3.0, -4.0, -6.0])


def pack_fp4(w):
    k, n = w.shape
    w = f64(np.asarray(w, np.float32).astype(ml_dtypes.bfloat16)).reshape(k // 32, 32, n)
    amax = np.abs(w).max(1)
    mant, ex = np.frexp(amax / 6.0)
    byte = np.clip(np.where(amax > 0, np.where(mant > 0.5, ex, ex - 1) + 127, 1), 1, 254)
    scaled = (w * np.exp2(127.0 - byte)[:, None, :]).reshape(k, n).astype(np.float32)
    c = np.ascontiguousarray(scaled.reshape(k // 512, 128, 4, n).transpose(0, 1, 3, 2)).astype(ml_dtypes.float4_e2m1fn).view(np.uint8) & 0xF
    words = (c[..., 0::2] | (c[..., 1::2] << 4)).reshape(k // 512, 128, 2 * n)
    return np.ascontiguousarray(words), np.ascontiguousarray(byte.astype(np.uint8).reshape(k // 512, 16, n))


def unpack_fp4(words, scales):
    g, _, n = scales.shape
    words = np.ascontiguousarray(words).reshape(g, 128, n, 2)
    nib = np.empty((g, 128, n, 4), np.uint8)
    nib[..., 0::2] = words & 0xF
    nib[..., 1::2] = words >> 4
    vals = E2M1[nib] * np.repeat(np.exp2(scales.astype(np.float64) - 127.0), 8, axis=1)[..., None]
    return vals.transpose(0, 1, 3, 2).reshape(g * 512, n)


def relu(v):
    return np.maximum(v, 0.0)


K, T, S, V, H, N = 512, 4096, 1024, 512, 512, 256


def setup_inputs():
    n = np.random.standard_normal
    s = mx_kscale(K)[:, None]
    u = mx_kscale(H)
    packed_w2 = pack_fp4(n((H, N)) / np.sqrt(2 * H) / u[:, None])
    packed_w3 = pack_fp4(n((H, N)) / np.sqrt(2 * H) / u[:, None])
    return {
        "xT": (n((K, T)) * s).astype(np.float32),
        "w1": (n((K, H)) / np.sqrt(K) / s * u).astype(np.float32),
        "w2_words": packed_w2[0],
        "w2_scales": packed_w2[1],
        "w3_words": packed_w3[0],
        "w3_scales": packed_w3[1],
        "offs": striped(np.random.permutation(T)[:S]),
        "cen": striped(np.random.permutation(S)[:V]),
        "pos1": striped(np.random.permutation(S)[:V]),
        "pos2": striped(np.random.permutation(S)[:V]),
    }


def reference(xT, w1, w2_words, w2_scales, w3_words, w3_scales, offs, cen, pos1, pos2):
    xq = mxq(f64(xT)[:, unstriped(offs)], 0, "e4m3")
    h = relu(mxq(f64(w1), 0, "e4m3").T @ xq)
    hc = h[:, unstriped(cen)]
    z = np.maximum(h[:, unstriped(pos1)], h[:, unstriped(pos2)])
    return relu(unpack_fp4(w2_words, w2_scales).T @ mxq(hc, 0, "e4m3") + unpack_fp4(w3_words, w3_scales).T @ mxq(z, 0, "e4m3"))

@@ -1,0 +1,231 @@
+from contextlib import ExitStack
+
+import concourse.mybir as mybir
+
+K, T, S, V, H, N = 512, 4096, 1024, 512, 512, 256
+FLOPS = 2 * K * H * S + 2 * 2 * H * N * V
+
+F32 = mybir.dt.float32
+BF16 = mybir.dt.bfloat16
+I32 = mybir.dt.int32
+U32 = mybir.dt.uint32
+U16 = mybir.dt.uint16
+U8 = mybir.dt.uint8
+FP8X4 = mybir.dt.float8_e4m3fn_x4
+FP4X4 = mybir.dt.float4_e2m1fn_x4
+RELU = mybir.ActivationFunctionType.Relu
+MAX = mybir.AluOpType.max
+
+P = 128
+PACK = 4
+PIECE = 128
+
+
+def tile_picked_sagecat_maxrelu_e_kernel(
+    tc, xT, w1, w2_words, w2_scales, w3_words, w3_scales, offs, cen, pos1, pos2, out
+):
+    nc = tc.nc
+    with ExitStack() as ctx:
+        keep = ctx.enter_context(tc.tile_pool(name="keep", bufs=1))
+        psum = ctx.enter_context(tc.psum_pool(name="psum", bufs=1))
+
+        def sb(name, cols, dtype, tag=None):
+            return keep.tile([P, cols], dtype, name=name, tag=tag or name, align_bytes=64)
+
+        def bank(b, name, cols):
+            return psum.tile([P, cols], F32, name=name, tag="bank%d" % b)
+
+        def quantize(codes, scales, values):
+            nc.vector.quantize_mx(out=codes.bitcast(FP8X4), scales=scales, in_=values)
+
+        offs_sb = keep.tile([P, S // 16], U16, name="offs_sb")
+        cen_sb = keep.tile([P, V // 16], U16, name="cen_sb")
+        pos1_sb = keep.tile([P, V // 16], U16, name="pos1_sb")
+        pos2_sb = keep.tile([P, V // 16], U16, name="pos2_sb")
+        x_rows = xT.rearrange("(p j) t -> p j t", j=PACK)
+        x_sb = [sb("x%d" % j, T, F32) for j in range(PACK)]
+        nc.sync.dma_start(out=x_sb[0][:], in_=x_rows[:, 0, :])
+        nc.sync.dma_start(offs_sb[:], offs)
+        for j in range(1, PACK):
+            nc.sync.dma_start(out=x_sb[j][:], in_=x_rows[:, j, :])
+        w1_rows = w1.rearrange("(p j) c -> p j c", j=PACK)
+        w1_raw = [sb("w1_raw%d" % u, PACK * H // 2, F32) for u in range(2)]
+        for u in range(2):
+            nc.sync.dma_start(
+                out=w1_raw[u][:].rearrange("p (j c) -> p j c", j=PACK),
+                in_=w1_rows[:, :, u * H // 2 : (u + 1) * H // 2],
+            )
+        nc.sync.dma_start(pos1_sb[:], pos1)
+        nc.sync.dma_start(pos2_sb[:], pos2)
+        nc.sync.dma_start(cen_sb[:], cen)
+        w3_sb = sb("w3_sb", 2 * N, U8)
+        w2_sb = sb("w2_sb", 2 * N, U8)
+        nc.sync.dma_start(out=w3_sb[:].bitcast(I32), in_=w3_words[0].bitcast(I32))
+        nc.sync.dma_start(out=w2_sb[:].bitcast(I32), in_=w2_words[0].bitcast(I32))
+        w23_scales = sb("w23_scales", 2 * N, U8)
+        nc.vector.memset(w23_scales[:].bitcast(I32), 0)
+        for a, rows in enumerate((w3_scales, w2_scales)):
+            for q in range(4):
+                nc.sync.dma_start(
+                    out=w23_scales[32 * q : 32 * q + 4, a * N : (a + 1) * N].bitcast(I32),
+                    in_=rows[0, 4 * q : 4 * q + 4, :].bitcast(I32),
+                )
+
+        half = S // 2
+        xg = [sb("xg%d" % u, PACK * half, BF16) for u in range(2)]
+        for j in range(PACK):
+            for u in range(2):
+                nc.vector.tensor_copy(
+                    xg[u][:].rearrange("p (n j) -> p n j", j=PACK)[:, :, j],
+                    x_sb[j][:].indirect(offs_sb[:, u * half // 16 : (u + 1) * half // 16]),
+                )
+
+        w1_bf = sb("w1_bf", PACK * H, BF16)
+        for u in range(2):
+            nc.scalar.copy(
+                w1_bf[:].rearrange("p (t m j) -> p m j t", t=PACK, j=PACK)[:, 64 * u : 64 * (u + 1)],
+                w1_raw[u][:].rearrange("p (j m t) -> p m j t", j=PACK, t=PACK),
+            )
+
+        xa_codes = sb("xa_codes", half, U32)
+        xa_scales = sb("xa_scales", half, U8)
+        xb_codes = sb("xb_codes", half, U32, tag="w1_raw1")
+        xb_scales = sb("xb_scales", half, U8)
+        w1_codes = sb("w1_codes", H, U32)
+        w1_scales = sb("w1_scales", H, U8)
+
+        def quantize_w1(lo, hi):
+            quantize(w1_codes[:, lo:hi], w1_scales[:, lo:hi], w1_bf[:, PACK * lo : PACK * hi])
+
+        quantize(xa_codes[:], xa_scales[:], xg[0][:])
+        quantize_w1(0, 128)
+        for lo in (0, 256):
+            quantize(xb_codes[:, lo : lo + 256], xb_scales[:, lo : lo + 256], xg[1][:, PACK * lo : PACK * (lo + 256)])
+        quantize_w1(128, 256)
+        quantize_w1(256, 512)
+
+        h = [sb("h%d" % t, S, F32) for t in range(PACK)]
+
+        def first_product(b, t, codes, scales, lo, cols, h_lo, on_vector):
+            acc = bank(b, "acc_h%d_%d" % (t, h_lo), cols)
+            nc.tensor.matmul_mx(
+                out=acc[:],
+                lhsT=w1_codes[:, P * t : P * (t + 1)].bitcast(FP8X4),
+                lhsT_scale=w1_scales[:, P * t : P * (t + 1)],
+                rhs=codes[:, lo : lo + cols].bitcast(FP8X4),
+                rhs_scale=scales[:, lo : lo + cols],
+                start=True,
+                stop=True,
+            )
+            if on_vector:
+                nc.vector.tensor_scalar_max(h[t][:, h_lo : h_lo + cols], acc[:], 0.0)
+            else:
+                nc.scalar.activation(h[t][:, h_lo : h_lo + cols], acc[:], RELU)
+
+        first_product(0, 0, xa_codes, xa_scales, 0, 512, 0, False)
+        first_product(1, 0, xb_codes, xb_scales, 0, 256, 512, False)
+        first_product(2, 0, xb_codes, xb_scales, 256, 256, 768, True)
+        for t in range(1, PACK):
+            first_product((2 * t + 1) % 8, t, xa_codes, xa_scales, 0, 512, 0, False)
+            first_product((2 * t + 2) % 8, t, xb_codes, xb_scales, 0, 512, 512, False)
+
+        n1 = sb("n1", PACK * V, BF16)
+        n2 = sb("n2", PACK * V, BF16)
+        for t in range(PACK):
+            for dst, lst in ((n1, pos1_sb), (n2, pos2_sb)):
+                nc.vector.tensor_copy(
+                    dst[:].rearrange("p (u t v) -> p u t v", u=2, t=PACK)[:, :, t, :],
+                    h[t][:].indirect(lst[:]),
+                )
+
+        def weave(dst, src):
+            nc.scalar.copy(
+                dst.rearrange("p (c i t) -> p c t i", i=4, t=PACK),
+                src.rearrange("p (t c i) -> p c t i", i=4, t=PACK),
+            )
+
+        z = sb("z", PACK * V, BF16)
+        z_w = sb("z_w", PACK * V, BF16)
+        for u in range(2):
+            run = slice(u * 1024, (u + 1) * 1024)
+            nc.vector.tensor_tensor(z[:, run], n1[:, run], n2[:, run], MAX)
+            weave(z_w[:, run], z[:, run])
+
+        c_w = sb("c_w", PACK * 3 * PIECE, BF16)
+        for t in range(PACK):
+            nc.vector.tensor_copy(
+                n1[:, 0:1024].rearrange("p (u t v) -> p u t v", u=2, t=PACK)[:, :, t, :],
+                h[t][:].indirect(cen_sb[:, 0:16]),
+            )
+        for r in range(2):
+            weave(c_w[:, 512 * r : 512 * (r + 1)], n1[:, 512 * r : 512 * (r + 1)])
+
+        z_codes = sb("z_codes", V, U32)
+        z_scales = sb("z_scales", V, U8)
+        for u in range(2):
+            quantize(z_codes[:, 256 * u : 256 * (u + 1)], z_scales[:, 256 * u : 256 * (u + 1)], z_w[:, 1024 * u : 1024 * (u + 1)])
+
+        accs = {}
+
+        def second_pass(r, m, w_sb, a, codes, scales, first):
+            nc.tensor.matmul_mx(
+                out=accs[r, m][:],
+                lhsT=w_sb[:, 2 * P * m : 2 * P * (m + 1)].bitcast(FP4X4),
+                lhsT_scale=w23_scales[:, a * N + P * m : a * N + P * (m + 1)],
+                rhs=codes[:, PIECE * r : PIECE * (r + 1)].bitcast(FP8X4),
+                rhs_scale=scales[:, PIECE * r : PIECE * (r + 1)],
+                start=first,
+                stop=not first,
+            )
+
+        for r in range(4):
+            for m in range(2):
+                accs[r, m] = bank((2 * r + m + 1) % 8, "acc_o%d_%d" % (r, m), PIECE)
+                second_pass(r, m, w3_sb, 0, z_codes, z_scales, True)
+
+        for t in range(PACK):
+            nc.vector.tensor_copy(
+                z_w[:, 0:512].rearrange("p (u t v) -> p u t v", u=2, t=PACK)[:, :, t, :],
+                h[t][:].indirect(cen_sb[:, 16:24]),
+            )
+        for u in range(2):
+            weave(c_w[:, 1024 + 256 * u : 1024 + 256 * (u + 1)], z_w[:, 256 * u : 256 * (u + 1)])
+
+        c_codes = sb("c_codes", V, U32)
+        c_scales = sb("c_scales", V, U8)
+        out_rows = out.rearrange("(m p) v -> p m v", p=P)
+        res = [sb("res%d" % g, 2 * w, F32) for g, w in enumerate((256, 128, 128))]
+
+        def quantize_c(r, lo):
+            quantize(c_codes[:, PIECE * r : PIECE * (r + 1)], c_scales[:, PIECE * r : PIECE * (r + 1)], c_w[:, lo : lo + 512])
+
+        def finish(r, dst, width, lo, vector_ms):
+            for m in range(2):
+                second_pass(r, m, w2_sb, 1, c_codes, c_scales, False)
+            for m in range(2):
+                cols = dst[:, m * width + lo : m * width + lo + PIECE]
+                if m in vector_ms:
+                    nc.vector.tensor_scalar_max(cols, accs[r, m][:], 0.0)
+                else:
+                    nc.scalar.activation(cols, accs[r, m][:], RELU)
+
+        def store(src, lo, width):
+            nc.sync.dma_start(out=out_rows[:, :, lo : lo + width], in_=src[:].rearrange("p (m v) -> p m v", m=2))
+
+        for r in range(2):
+            quantize_c(r, 512 * r)
+        for r in range(2):
+            finish(r, res[0], 256, PIECE * r, ())
+        store(res[0], 0, 256)
+
+        for t in range(PACK):
+            nc.vector.tensor_copy(
+                c_w[:, 0:512].rearrange("p (n t) -> p n t", t=PACK)[:, :, t],
+                h[t][:].indirect(cen_sb[:, 24:32]),
+            )
+        quantize_c(2, 1024)
+        quantize_c(3, 0)
+        finish(2, res[1], 128, 0, ())
+        store(res[1], 256, 128)
+        finish(3, res[2], 128, 0, (0, 1))
+        store(res[2], 384, 128)

@@ -49,11 +49,12 @@ def tile_picked_sagecat_maxrelu_e_kernel(
         for j in range(1, PACK):
             nc.sync.dma_start(out=x_sb[j][:], in_=x_rows[:, j, :])
         w1_rows = w1.rearrange("(p j) c -> p j c", j=PACK)
-        w1_raw = [sb("w1_raw%d" % u, PACK * H // 2, F32) for u in range(2)]
-        for u in range(2):
+        w1_cuts = (0, 256, 480, 512)
+        w1_raw = [sb("w1_raw%d" % u, PACK * (w1_cuts[u + 1] - w1_cuts[u]), F32) for u in range(3)]
+        for u in range(3):
             nc.sync.dma_start(
                 out=w1_raw[u][:].rearrange("p (j c) -> p j c", j=PACK),
-                in_=w1_rows[:, :, u * H // 2 : (u + 1) * H // 2],
+                in_=w1_rows[:, :, w1_cuts[u] : w1_cuts[u + 1]],
             )
         nc.sync.dma_start(pos1_sb[:], pos1)
         nc.sync.dma_start(pos2_sb[:], pos2)
@@ -81,15 +82,20 @@ def tile_picked_sagecat_maxrelu_e_kernel(
                 )
 
         w1_bf = sb("w1_bf", PACK * H, BF16)
-        for u in range(2):
-            nc.scalar.copy(
-                w1_bf[:].rearrange("p (t m j) -> p m j t", t=PACK, j=PACK)[:, 64 * u : 64 * (u + 1)],
-                w1_raw[u][:].rearrange("p (j m t) -> p m j t", j=PACK, t=PACK),
-            )
+        def deal_w1(u, ts):
+            dealt = w1_bf[:].rearrange("p (t m j) -> p m j t", t=PACK, j=PACK)[:, w1_cuts[u] // PACK : w1_cuts[u + 1] // PACK]
+            raw = w1_raw[u][:].rearrange("p (j m t) -> p m j t", j=PACK, t=PACK)
+            nc.scalar.copy(dealt[:, :, :, ts], raw[:, :, :, ts])
+
+        deal_w1(0, 0)
+        deal_w1(1, 0)
+        deal_w1(2, slice(0, PACK))
+        deal_w1(0, slice(1, PACK))
+        deal_w1(1, slice(1, PACK))
 
         xa_codes = sb("xa_codes", half, U32)
         xa_scales = sb("xa_scales", half, U8)
-        xb_codes = sb("xb_codes", half, U32, tag="w1_raw1")
+        xb_codes = sb("xb_codes", half, U32, tag="w1_raw2")
         xb_scales = sb("xb_scales", half, U8)
         w1_codes = sb("w1_codes", H, U32)
         w1_scales = sb("w1_scales", H, U8)
@@ -123,8 +129,8 @@ def tile_picked_sagecat_maxrelu_e_kernel(
                 nc.scalar.activation(h[t][:, h_lo : h_lo + cols], acc[:], RELU)
 
         first_product(0, 0, xa_codes, xa_scales, 0, 512, 0, False)
-        first_product(1, 0, xb_codes, xb_scales, 0, 256, 512, False)
-        first_product(2, 0, xb_codes, xb_scales, 256, 256, 768, True)
+        first_product(1, 0, xb_codes, xb_scales, 0, 256, 512, True)
+        first_product(2, 0, xb_codes, xb_scales, 256, 256, 768, False)
         for t in range(1, PACK):
             first_product((2 * t + 1) % 8, t, xa_codes, xa_scales, 0, 512, 0, False)
             first_product((2 * t + 2) % 8, t, xb_codes, xb_scales, 0, 512, 512, False)
@@ -225,7 +231,7 @@ def tile_picked_sagecat_maxrelu_e_kernel(
             )
         quantize_c(2, 1024)
         quantize_c(3, 0)
-        finish(2, res[1], 128, 0, ())
+        finish(2, res[1], 128, 0, (1,))
         store(res[1], 256, 128)
-        finish(3, res[2], 128, 0, (0, 1))
+        finish(3, res[2], 128, 0, (1,))
         store(res[2], 384, 128)

@@ -93,56 +93,67 @@ def tile_picked_sagecat_maxrelu_e_kernel(
         deal_w1(0, slice(1, PACK))
         deal_w1(1, slice(1, PACK))
 
-        xa_codes = sb("xa_codes", half, U32)
-        xa_scales = sb("xa_scales", half, U8)
-        xb_codes = sb("xb_codes", half, U32, tag="w1_raw2")
-        xb_scales = sb("xb_scales", half, U8)
+        xa_codes = sb("xa_codes", 256, U32)
+        xb_codes = sb("xb_codes", 768, U32, tag="w1_raw2")
+        x_scales = sb("x_scales", S, U8)
         w1_codes = sb("w1_codes", H, U32)
         w1_scales = sb("w1_scales", H, U8)
 
         def quantize_w1(lo, hi):
             quantize(w1_codes[:, lo:hi], w1_scales[:, lo:hi], w1_bf[:, PACK * lo : PACK * hi])
 
-        quantize(xa_codes[:], xa_scales[:], xg[0][:])
+        def x_codes(lo, hi):
+            return xa_codes[:, lo:hi] if hi <= 256 else xb_codes[:, lo - 256 : hi - 256]
+
+        def quantize_x(lo):
+            quantize(x_codes(lo, lo + 256), x_scales[:, lo : lo + 256], xg[lo // half][:, PACK * (lo % half) : PACK * (lo % half + 256)])
+
+        quantize_x(0)
         quantize_w1(0, 128)
-        for lo in (0, 256):
-            quantize(xb_codes[:, lo : lo + 256], xb_scales[:, lo : lo + 256], xg[1][:, PACK * lo : PACK * (lo + 256)])
+        for lo in (256, 512, 768):
+            quantize_x(lo)
         quantize_w1(128, 256)
         quantize_w1(256, 512)
 
         h = [sb("h%d" % t, S, F32) for t in range(PACK)]
 
-        def first_product(b, t, codes, scales, lo, cols, h_lo, on_vector):
-            acc = bank(b, "acc_h%d_%d" % (t, h_lo), cols)
+        def product(acc, t, lo, hi):
             nc.tensor.matmul_mx(
-                out=acc[:],
+                out=acc,
                 lhsT=w1_codes[:, P * t : P * (t + 1)].bitcast(FP8X4),
                 lhsT_scale=w1_scales[:, P * t : P * (t + 1)],
-                rhs=codes[:, lo : lo + cols].bitcast(FP8X4),
-                rhs_scale=scales[:, lo : lo + cols],
+                rhs=x_codes(lo, hi).bitcast(FP8X4),
+                rhs_scale=x_scales[:, lo:hi],
                 start=True,
                 stop=True,
             )
-            if on_vector:
-                nc.vector.tensor_scalar_max(h[t][:, h_lo : h_lo + cols], acc[:], 0.0)
-            else:
-                nc.scalar.activation(h[t][:, h_lo : h_lo + cols], acc[:], RELU)
 
-        first_product(0, 0, xa_codes, xa_scales, 0, 512, 0, False)
-        first_product(1, 0, xb_codes, xb_scales, 0, 256, 512, True)
-        first_product(2, 0, xb_codes, xb_scales, 256, 256, 768, False)
+        for r in range(4):
+            acc = bank(r, "acc_h0_%d" % r, 256)
+            product(acc[:], 0, 256 * r, 256 * (r + 1))
+            if r == 2:
+                nc.vector.tensor_scalar_max(h[0][:, 256 * r : 256 * (r + 1)], acc[:], 0.0)
+            else:
+                nc.scalar.activation(h[0][:, 256 * r : 256 * (r + 1)], acc[:], RELU)
         for t in range(1, PACK):
-            first_product((2 * t + 1) % 8, t, xa_codes, xa_scales, 0, 512, 0, False)
-            first_product((2 * t + 2) % 8, t, xb_codes, xb_scales, 0, 512, 512, False)
+            acc = bank((2 * t + 2) % 8, "acc_h%d_0" % t, 512)
+            product(acc[:, 0:256], t, 0, 256)
+            product(acc[:, 256:512], t, 256, 512)
+            nc.scalar.activation(h[t][:, 0:512], acc[:], RELU)
+            acc = bank((2 * t + 3) % 8, "acc_h%d_1" % t, 512)
+            product(acc[:], t, 512, 1024)
+            nc.scalar.activation(h[t][:, 512:1024], acc[:], RELU)
 
         n1 = sb("n1", PACK * V, BF16)
         n2 = sb("n2", PACK * V, BF16)
         for t in range(PACK):
             for dst, lst in ((n1, pos1_sb), (n2, pos2_sb)):
-                nc.vector.tensor_copy(
-                    dst[:].rearrange("p (u t v) -> p u t v", u=2, t=PACK)[:, :, t, :],
-                    h[t][:].indirect(lst[:]),
-                )
+                planes = dst[:].rearrange("p (r t v) -> p r t v", r=4, t=PACK)
+                if t == PACK - 1 and dst is n2:
+                    for u in range(2):
+                        nc.vector.tensor_copy(planes[:, 2 * u : 2 * u + 2, t, :], h[t][:].indirect(lst[:, 16 * u : 16 * (u + 1)]))
+                else:
+                    nc.vector.tensor_copy(planes[:, :, t, :], h[t][:].indirect(lst[:]))
 
         def weave(dst, src):
             nc.scalar.copy(
@@ -155,7 +166,10 @@ def tile_picked_sagecat_maxrelu_e_kernel(
         for u in range(2):
             run = slice(u * 1024, (u + 1) * 1024)
             nc.vector.tensor_tensor(z[:, run], n1[:, run], n2[:, run], MAX)
-            weave(z_w[:, run], z[:, run])
+            nc.scalar.copy(
+                z_w[:, run].rearrange("p (r c i t) -> p r c t i", r=2, i=4, t=PACK),
+                z[:, run].rearrange("p (r t c i) -> p r c t i", r=2, i=4, t=PACK),
+            )
 
         c_w = sb("c_w", PACK * 3 * PIECE, BF16)
         for t in range(PACK):
@@ -186,7 +200,7 @@ def tile_picked_sagecat_maxrelu_e_kernel(
 
         for r in range(4):
             for m in range(2):
-                accs[r, m] = bank((2 * r + m + 1) % 8, "acc_o%d_%d" % (r, m), PIECE)
+                accs[r, m] = bank((2 * r + m + 2) % 8, "acc_o%d_%d" % (r, m), PIECE)
                 second_pass(r, m, w3_sb, 0, z_codes, z_scales, True)
 
         for t in range(PACK):

@@ -15,6 +15,8 @@ FP8X4 = mybir.dt.float8_e4m3fn_x4
 FP4X4 = mybir.dt.float4_e2m1fn_x4
 RELU = mybir.ActivationFunctionType.Relu
 MAX = mybir.AluOpType.max
+ADD = mybir.AluOpType.add
+SUB = mybir.AluOpType.subtract
 
 P = 128
 PACK = 4
@@ -27,6 +29,7 @@ def tile_picked_sagecat_maxrelu_e_kernel(
     nc = tc.nc
     with ExitStack() as ctx:
         keep = ctx.enter_context(tc.tile_pool(name="keep", bufs=1))
+        late = ctx.enter_context(tc.tile_pool(name="late", bufs=1))
         psum = ctx.enter_context(tc.psum_pool(name="psum", bufs=1))
 
         def sb(name, cols, dtype, tag=None):
@@ -146,14 +149,18 @@ def tile_picked_sagecat_maxrelu_e_kernel(
 
         n1 = sb("n1", PACK * V, BF16)
         n2 = sb("n2", PACK * V, BF16)
-        for t in range(PACK):
-            for dst, lst in ((n1, pos1_sb), (n2, pos2_sb)):
-                planes = dst[:].rearrange("p (r t v) -> p r t v", r=4, t=PACK)
-                if t == PACK - 1 and dst is n2:
-                    for u in range(2):
-                        nc.vector.tensor_copy(planes[:, 2 * u : 2 * u + 2, t, :], h[t][:].indirect(lst[:, 16 * u : 16 * (u + 1)]))
-                else:
-                    nc.vector.tensor_copy(planes[:, :, t, :], h[t][:].indirect(lst[:]))
+        ca = sb("ca", 1024, BF16)
+        z0 = sb("z0", 1024, BF16)
+        z1 = late.tile([P, 1024], BF16, name="z1", offset=0, align_bytes=64)
+        zs = (z0, z1)
+        diff = [sb("diff%d" % t, V, F32) for t in range(2)]
+        gain = [sb("gain%d" % t, V, F32) for t in range(2)]
+
+        def plane(tile, t):
+            return tile[:].rearrange("p (r t v) -> p r t v", t=PACK, v=PIECE)[:, :, t, :]
+
+        def runs(ap):
+            return ap.rearrange("p (r v) -> p r v", v=PIECE)
 
         def weave(dst, src):
             nc.scalar.copy(
@@ -161,67 +168,79 @@ def tile_picked_sagecat_maxrelu_e_kernel(
                 src.rearrange("p (t c i) -> p c t i", i=4, t=PACK),
             )
 
-        z = sb("z", PACK * V, BF16)
+        for t in range(PACK):
+            nc.vector.tensor_copy(plane(ca, t), h[t][:].indirect(cen_sb[:, 0:16]))
+            nc.vector.tensor_copy(plane(n1, t), h[t][:].indirect(pos1_sb[:]))
+            if t == PACK - 1:
+                for u in range(2):
+                    nc.vector.tensor_copy(plane(n2, t)[:, 2 * u : 2 * u + 2, :], h[t][:].indirect(pos2_sb[:, 16 * u : 16 * (u + 1)]))
+            else:
+                nc.vector.tensor_copy(plane(n2, t), h[t][:].indirect(pos2_sb[:]))
+            if t < 2:
+                nc.gpsimd.tensor_tensor(runs(diff[t][:]), plane(n1, t), plane(n2, t), SUB)
+                nc.scalar.activation(gain[t][:], diff[t][:], RELU)
+                for u in range(2):
+                    nc.gpsimd.tensor_tensor(
+                        plane(zs[u], t), runs(gain[t][:, 256 * u : 256 * (u + 1)]), plane(n2, t)[:, 2 * u : 2 * u + 2, :], ADD
+                    )
+        ca_w = sb("ca_w", 1024, BF16)
+        for r in range(2):
+            weave(ca_w[:, 512 * r : 512 * (r + 1)], ca[:, 512 * r : 512 * (r + 1)])
+
         z_w = sb("z_w", PACK * V, BF16)
         for u in range(2):
             run = slice(u * 1024, (u + 1) * 1024)
-            nc.vector.tensor_tensor(z[:, run], n1[:, run], n2[:, run], MAX)
+            upper = [ap.rearrange("p (r t v) -> p r t v", r=2, t=2)[:, :, 1, :] for ap in (zs[u][:], n1[:, run], n2[:, run])]
+            nc.vector.tensor_tensor(upper[0], upper[1], upper[2], MAX)
             nc.scalar.copy(
                 z_w[:, run].rearrange("p (r c i t) -> p r c t i", r=2, i=4, t=PACK),
-                z[:, run].rearrange("p (r t c i) -> p r c t i", r=2, i=4, t=PACK),
+                zs[u][:].rearrange("p (r t c i) -> p r c t i", r=2, i=4, t=PACK),
             )
-
-        c_w = sb("c_w", PACK * 3 * PIECE, BF16)
-        for t in range(PACK):
-            nc.vector.tensor_copy(
-                n1[:, 0:1024].rearrange("p (u t v) -> p u t v", u=2, t=PACK)[:, :, t, :],
-                h[t][:].indirect(cen_sb[:, 0:16]),
-            )
-        for r in range(2):
-            weave(c_w[:, 512 * r : 512 * (r + 1)], n1[:, 512 * r : 512 * (r + 1)])
-
-        z_codes = sb("z_codes", V, U32)
-        z_scales = sb("z_scales", V, U8)
-        for u in range(2):
-            quantize(z_codes[:, 256 * u : 256 * (u + 1)], z_scales[:, 256 * u : 256 * (u + 1)], z_w[:, 1024 * u : 1024 * (u + 1)])
-
-        accs = {}
-
-        def second_pass(r, m, w_sb, a, codes, scales, first):
-            nc.tensor.matmul_mx(
-                out=accs[r, m][:],
-                lhsT=w_sb[:, 2 * P * m : 2 * P * (m + 1)].bitcast(FP4X4),
-                lhsT_scale=w23_scales[:, a * N + P * m : a * N + P * (m + 1)],
-                rhs=codes[:, PIECE * r : PIECE * (r + 1)].bitcast(FP8X4),
-                rhs_scale=scales[:, PIECE * r : PIECE * (r + 1)],
-                start=first,
-                stop=not first,
-            )
-
-        for r in range(4):
-            for m in range(2):
-                accs[r, m] = bank((2 * r + m + 2) % 8, "acc_o%d_%d" % (r, m), PIECE)
-                second_pass(r, m, w3_sb, 0, z_codes, z_scales, True)
 
         for t in range(PACK):
             nc.vector.tensor_copy(
-                z_w[:, 0:512].rearrange("p (u t v) -> p u t v", u=2, t=PACK)[:, :, t, :],
+                n1[:, 0:512].rearrange("p (u t v) -> p u t v", u=2, t=PACK)[:, :, t, :],
                 h[t][:].indirect(cen_sb[:, 16:24]),
             )
+        cb_w = late.tile([P, 512], BF16, name="cb_w", offset=0, align_bytes=64)
         for u in range(2):
-            weave(c_w[:, 1024 + 256 * u : 1024 + 256 * (u + 1)], z_w[:, 256 * u : 256 * (u + 1)])
+            weave(cb_w[:, 256 * u : 256 * (u + 1)], n1[:, 256 * u : 256 * (u + 1)])
 
-        c_codes = sb("c_codes", V, U32)
+        c_codes = sb("c_codes", 3 * PIECE, U32)
+        cc_codes = late.tile([P, PIECE], U32, name="cc_codes", offset=1024, align_bytes=64)
         c_scales = sb("c_scales", V, U8)
+        z_codes = sb("z_codes", V, U32)
+        z_scales = sb("z_scales", V, U8)
         out_rows = out.rearrange("(m p) v -> p m v", p=P)
         res = [sb("res%d" % g, 2 * w, F32) for g, w in enumerate((256, 128, 128))]
+        accs = {}
 
-        def quantize_c(r, lo):
-            quantize(c_codes[:, PIECE * r : PIECE * (r + 1)], c_scales[:, PIECE * r : PIECE * (r + 1)], c_w[:, lo : lo + 512])
+        def c_piece(r):
+            return cc_codes[:] if r == 3 else c_codes[:, PIECE * r : PIECE * (r + 1)]
+
+        def second_pass(r, centre, first):
+            cols = slice(PIECE * r, PIECE * (r + 1))
+            w_sb, a = (w2_sb, 1) if centre else (w3_sb, 0)
+            for m in range(2):
+                if first:
+                    accs[r, m] = bank((2 * r + m + 2) % 8, "acc_o%d_%d" % (r, m), PIECE)
+                nc.tensor.matmul_mx(
+                    out=accs[r, m][:],
+                    lhsT=w_sb[:, 2 * P * m : 2 * P * (m + 1)].bitcast(FP4X4),
+                    lhsT_scale=w23_scales[:, a * N + P * m : a * N + P * (m + 1)],
+                    rhs=(c_piece(r) if centre else z_codes[:, cols]).bitcast(FP8X4),
+                    rhs_scale=(c_scales if centre else z_scales)[:, cols],
+                    start=first,
+                    stop=not first,
+                )
+
+        def quantize_c(r, values):
+            quantize(c_piece(r), c_scales[:, PIECE * r : PIECE * (r + 1)], values)
+
+        def quantize_z(u):
+            quantize(z_codes[:, 256 * u : 256 * (u + 1)], z_scales[:, 256 * u : 256 * (u + 1)], z_w[:, 1024 * u : 1024 * (u + 1)])
 
         def finish(r, dst, width, lo, vector_ms):
-            for m in range(2):
-                second_pass(r, m, w2_sb, 1, c_codes, c_scales, False)
             for m in range(2):
                 cols = dst[:, m * width + lo : m * width + lo + PIECE]
                 if m in vector_ms:
@@ -232,20 +251,26 @@ def tile_picked_sagecat_maxrelu_e_kernel(
         def store(src, lo, width):
             nc.sync.dma_start(out=out_rows[:, :, lo : lo + width], in_=src[:].rearrange("p (m v) -> p m v", m=2))
 
+        quantize(c_codes[:, 0:256], c_scales[:, 0:256], ca_w[:])
         for r in range(2):
-            quantize_c(r, 512 * r)
+            second_pass(r, True, True)
+        quantize_z(0)
         for r in range(2):
+            second_pass(r, False, False)
             finish(r, res[0], 256, PIECE * r, ())
         store(res[0], 0, 256)
 
         for t in range(PACK):
             nc.vector.tensor_copy(
-                c_w[:, 0:512].rearrange("p (n t) -> p n t", t=PACK)[:, :, t],
+                z0[:, 0:512].rearrange("p (n t) -> p n t", t=PACK)[:, :, t],
                 h[t][:].indirect(cen_sb[:, 24:32]),
             )
-        quantize_c(2, 1024)
-        quantize_c(3, 0)
-        finish(2, res[1], 128, 0, (1,))
-        store(res[1], 256, 128)
-        finish(3, res[2], 128, 0, (1,))
-        store(res[2], 384, 128)
+        quantize_z(1)
+        for r in (3, 2):
+            second_pass(r, False, True)
+        quantize_c(3, z0[:, 0:512])
+        quantize_c(2, cb_w[:])
+        for r in (3, 2):
+            second_pass(r, True, False)
+            finish(r, res[r - 1], 128, 0, (1,))
+            store(res[r - 1], PIECE * r, 128)

@@ -169,7 +169,8 @@ def tile_picked_sagecat_maxrelu_e_kernel(
             )
 
         for t in range(PACK):
-            nc.vector.tensor_copy(plane(ca, t), h[t][:].indirect(cen_sb[:, 0:16]))
+            if t >= 2:
+                nc.vector.tensor_copy(plane(ca, t), h[t][:].indirect(cen_sb[:, 0:16]))
             nc.vector.tensor_copy(plane(n1, t), h[t][:].indirect(pos1_sb[:]))
             if t == PACK - 1:
                 for u in range(2):
@@ -177,8 +178,12 @@ def tile_picked_sagecat_maxrelu_e_kernel(
             else:
                 nc.vector.tensor_copy(plane(n2, t), h[t][:].indirect(pos2_sb[:]))
             if t < 2:
-                nc.gpsimd.tensor_tensor(runs(diff[t][:]), plane(n1, t), plane(n2, t), SUB)
-                nc.scalar.activation(gain[t][:], diff[t][:], RELU)
+                nc.vector.tensor_copy(plane(ca, t), h[t][:].indirect(cen_sb[:, 0:16]))
+                for u in range(2):
+                    cols = slice(256 * u, 256 * (u + 1))
+                    pair = slice(2 * u, 2 * u + 2)
+                    nc.gpsimd.tensor_tensor(runs(diff[t][:, cols]), plane(n1, t)[:, pair, :], plane(n2, t)[:, pair, :], SUB)
+                    nc.scalar.activation(gain[t][:, cols], diff[t][:, cols], RELU)
                 for u in range(2):
                     nc.gpsimd.tensor_tensor(
                         plane(zs[u], t), runs(gain[t][:, 256 * u : 256 * (u + 1)]), plane(n2, t)[:, 2 * u : 2 * u + 2, :], ADD

@@ -108,13 +108,15 @@ def tile_picked_sagecat_maxrelu_e_kernel(
         def x_codes(lo, hi):
             return xa_codes[:, lo:hi] if hi <= 256 else xb_codes[:, lo - 256 : hi - 256]
 
-        def quantize_x(lo):
-            quantize(x_codes(lo, lo + 256), x_scales[:, lo : lo + 256], xg[lo // half][:, PACK * (lo % half) : PACK * (lo % half + 256)])
+        def quantize_x(lo, hi):
+            quantize(x_codes(lo, hi), x_scales[:, lo:hi], xg[lo // half][:, PACK * (lo % half) : PACK * (lo % half + hi - lo)])
 
-        quantize_x(0)
+        x_cuts = (0, 256, 512, 768, 896, 1024)
+        x_runs = list(zip(x_cuts, x_cuts[1:]))
+        quantize_x(0, 256)
         quantize_w1(0, 128)
-        for lo in (256, 512, 768):
-            quantize_x(lo)
+        for lo, hi in x_runs[1:]:
+            quantize_x(lo, hi)
         quantize_w1(128, 256)
         quantize_w1(256, 512)
 
@@ -131,19 +133,19 @@ def tile_picked_sagecat_maxrelu_e_kernel(
                 stop=True,
             )
 
-        for r in range(4):
-            acc = bank(r, "acc_h0_%d" % r, 256)
-            product(acc[:], 0, 256 * r, 256 * (r + 1))
+        for r, (lo, hi) in enumerate(x_runs):
+            acc = bank(r, "acc_h0_%d" % r, hi - lo)
+            product(acc[:], 0, lo, hi)
             if r == 2:
-                nc.vector.tensor_scalar_max(h[0][:, 256 * r : 256 * (r + 1)], acc[:], 0.0)
+                nc.vector.tensor_scalar_max(h[0][:, lo:hi], acc[:], 0.0)
             else:
-                nc.scalar.activation(h[0][:, 256 * r : 256 * (r + 1)], acc[:], RELU)
+                nc.scalar.activation(h[0][:, lo:hi], acc[:], RELU)
         for t in range(1, PACK):
-            acc = bank((2 * t + 2) % 8, "acc_h%d_0" % t, 512)
+            acc = bank((2 * t + 3) % 8, "acc_h%d_0" % t, 512)
             product(acc[:, 0:256], t, 0, 256)
             product(acc[:, 256:512], t, 256, 512)
             nc.scalar.activation(h[t][:, 0:512], acc[:], RELU)
-            acc = bank((2 * t + 3) % 8, "acc_h%d_1" % t, 512)
+            acc = bank((2 * t + 4) % 8, "acc_h%d_1" % t, 512)
             product(acc[:], t, 512, 1024)
             nc.scalar.activation(h[t][:, 512:1024], acc[:], RELU)
 
@@ -202,15 +204,6 @@ def tile_picked_sagecat_maxrelu_e_kernel(
                 zs[u][:].rearrange("p (r t c i) -> p r c t i", r=2, i=4, t=PACK),
             )
 
-        for t in range(PACK):
-            nc.vector.tensor_copy(
-                n1[:, 0:512].rearrange("p (u t v) -> p u t v", u=2, t=PACK)[:, :, t, :],
-                h[t][:].indirect(cen_sb[:, 16:24]),
-            )
-        cb_w = late.tile([P, 512], BF16, name="cb_w", offset=0, align_bytes=64)
-        for u in range(2):
-            weave(cb_w[:, 256 * u : 256 * (u + 1)], n1[:, 256 * u : 256 * (u + 1)])
-
         c_codes = sb("c_codes", 3 * PIECE, U32)
         cc_codes = late.tile([P, PIECE], U32, name="cc_codes", offset=1024, align_bytes=64)
         c_scales = sb("c_scales", V, U8)
@@ -253,15 +246,40 @@ def tile_picked_sagecat_maxrelu_e_kernel(
                 else:
                     nc.scalar.activation(cols, accs[r, m][:], RELU)
 
+        def warm(count, first_bank, codes, scales):
+            for i in range(count):
+                spare = bank(first_bank + i % 2, "spare%d_%d" % (first_bank, i), 256)
+                nc.tensor.matmul_mx(
+                    out=spare[:],
+                    lhsT=w1_codes[:, 0:P].bitcast(FP8X4),
+                    lhsT_scale=w1_scales[:, 0:P],
+                    rhs=codes[:, 0:256].bitcast(FP8X4),
+                    rhs_scale=scales[:, 0:256],
+                    start=True,
+                    stop=True,
+                )
+
         def store(src, lo, width):
             nc.sync.dma_start(out=out_rows[:, :, lo : lo + width], in_=src[:].rearrange("p (m v) -> p m v", m=2))
 
         quantize(c_codes[:, 0:256], c_scales[:, 0:256], ca_w[:])
         for r in range(2):
             second_pass(r, True, True)
+        warm(3, 6, c_codes, c_scales)
+        for t in range(PACK):
+            nc.vector.tensor_copy(
+                ca[:, 512:1024].rearrange("p (u t v) -> p u t v", u=2, t=PACK)[:, :, t, :],
+                h[t][:].indirect(cen_sb[:, 16:24]),
+            )
+        cb_w = late.tile([P, 512], BF16, name="cb_w", offset=0, align_bytes=64)
+        for u in range(2):
+            weave(cb_w[:, 256 * u : 256 * (u + 1)], ca[:, 512 + 256 * u : 512 + 256 * (u + 1)])
+
         quantize_z(0)
         for r in range(2):
             second_pass(r, False, False)
+        warm(2, 0, z_codes, z_scales)
+        for r in range(2):
             finish(r, res[0], 256, PIECE * r, ())
         store(res[0], 0, 256)
 

@@ -52,7 +52,7 @@ def tile_picked_sagecat_maxrelu_e_kernel(
         for j in range(1, PACK):
             nc.sync.dma_start(out=x_sb[j][:], in_=x_rows[:, j, :])
         w1_rows = w1.rearrange("(p j) c -> p j c", j=PACK)
-        w1_cuts = (0, 256, 480, 512)
+        w1_cuts = (0, 320, 480, 512)
         w1_raw = [sb("w1_raw%d" % u, PACK * (w1_cuts[u + 1] - w1_cuts[u]), F32) for u in range(3)]
         for u in range(3):
             nc.sync.dma_start(

@@ -29,7 +29,6 @@ def tile_picked_sagecat_maxrelu_e_kernel(
     nc = tc.nc
     with ExitStack() as ctx:
         keep = ctx.enter_context(tc.tile_pool(name="keep", bufs=1))
-        late = ctx.enter_context(tc.tile_pool(name="late", bufs=1))
         psum = ctx.enter_context(tc.psum_pool(name="psum", bufs=1))
 
         def sb(name, cols, dtype, tag=None):
@@ -151,70 +150,55 @@ def tile_picked_sagecat_maxrelu_e_kernel(
 
         n1 = sb("n1", PACK * V, BF16)
         n2 = sb("n2", PACK * V, BF16)
-        ca = sb("ca", 1024, BF16)
-        z0 = sb("z0", 1024, BF16)
-        z1 = late.tile([P, 1024], BF16, name="z1", offset=0, align_bytes=64)
-        zs = (z0, z1)
-        diff = [sb("diff%d" % t, V, F32) for t in range(2)]
+        z01 = sb("z01", 2 * V, BF16)
+        mix = sb("mix", 2560, BF16)
+        diff = [sb("diff0", V, F32), None]
         gain = [sb("gain%d" % t, V, F32) for t in range(2)]
+        z_w = sb("z_w", PACK * V, BF16)
+        stage_a = mix[:, 496:1520]
+        stage_b = mix[:, 2032:2544]
+        z23 = (mix[:, 992:1504], mix[:, 1504:2016])
+        c_late = (mix[:, 0:512], mix[:, 512:1024])
 
         def plane(tile, t):
-            return tile[:].rearrange("p (r t v) -> p r t v", t=PACK, v=PIECE)[:, :, t, :]
+            return tile[:, V * t : V * (t + 1)]
 
-        def runs(ap):
-            return ap.rearrange("p (r v) -> p r v", v=PIECE)
+        def woven(dst, planes):
+            return dst.rearrange("p (c i t) -> p c t i", i=4, t=PACK)[:, :, planes, :]
 
-        def weave(dst, src):
-            nc.scalar.copy(
-                dst.rearrange("p (c i t) -> p c t i", i=4, t=PACK),
-                src.rearrange("p (t c i) -> p c t i", i=4, t=PACK),
-            )
+        def by_plane(src, count):
+            return src.rearrange("p (t c i) -> p c t i", i=4, t=count)
 
         for t in range(PACK):
-            if t >= 2:
-                nc.vector.tensor_copy(plane(ca, t), h[t][:].indirect(cen_sb[:, 0:16]))
+            if t == 3:
+                nc.vector.tensor_copy(stage_a[:, 256 * t : 256 * (t + 1)], h[t][:].indirect(cen_sb[:, 0:16]))
             nc.vector.tensor_copy(plane(n1, t), h[t][:].indirect(pos1_sb[:]))
-            if t == PACK - 1:
-                for u in range(2):
-                    nc.vector.tensor_copy(plane(n2, t)[:, 2 * u : 2 * u + 2, :], h[t][:].indirect(pos2_sb[:, 16 * u : 16 * (u + 1)]))
-            else:
-                nc.vector.tensor_copy(plane(n2, t), h[t][:].indirect(pos2_sb[:]))
+            nc.vector.tensor_copy(plane(n2, t), h[t][:].indirect(pos2_sb[:]))
+            if t == 2:
+                nc.vector.tensor_copy(stage_a[:, 256 * t : 256 * (t + 1)], h[t][:].indirect(cen_sb[:, 0:16]))
             if t < 2:
-                nc.vector.tensor_copy(plane(ca, t), h[t][:].indirect(cen_sb[:, 0:16]))
+                both = mix[:, 496:2544].rearrange("p (a v) -> p a v", v=256)[:, t : t + 7 : 6, :]
+                nc.vector.tensor_copy(both, h[t][:].indirect(cen_sb[:]))
+                if t == 1:
+                    diff[1] = sb("diff1", V, F32, tag="gain0")
                 for u in range(2):
                     cols = slice(256 * u, 256 * (u + 1))
-                    pair = slice(2 * u, 2 * u + 2)
-                    nc.gpsimd.tensor_tensor(runs(diff[t][:, cols]), plane(n1, t)[:, pair, :], plane(n2, t)[:, pair, :], SUB)
+                    nc.gpsimd.tensor_tensor(diff[t][:, cols], plane(n1, t)[:, cols], plane(n2, t)[:, cols], SUB)
                     nc.scalar.activation(gain[t][:, cols], diff[t][:, cols], RELU)
                 for u in range(2):
-                    nc.gpsimd.tensor_tensor(
-                        plane(zs[u], t), runs(gain[t][:, 256 * u : 256 * (u + 1)]), plane(n2, t)[:, 2 * u : 2 * u + 2, :], ADD
-                    )
-        ca_w = sb("ca_w", 1024, BF16)
-        for r in range(2):
-            weave(ca_w[:, 512 * r : 512 * (r + 1)], ca[:, 512 * r : 512 * (r + 1)])
+                    cols = slice(256 * u, 256 * (u + 1))
+                    nc.gpsimd.tensor_tensor(plane(z01, t)[:, cols], gain[t][:, cols], plane(n2, t)[:, cols], ADD)
+        nc.scalar.copy(woven(z_w[:], slice(0, 2)), by_plane(z01[:], 2))
+        ca_w = sb("ca_w", 1024, BF16, tag="z01")
+        nc.scalar.copy(woven(ca_w[:], slice(0, PACK)), by_plane(stage_a, PACK))
 
-        z_w = sb("z_w", PACK * V, BF16)
-        for u in range(2):
-            run = slice(u * 1024, (u + 1) * 1024)
-            upper = [ap.rearrange("p (r t v) -> p r t v", r=2, t=2)[:, :, 1, :] for ap in (zs[u][:], n1[:, run], n2[:, run])]
-            nc.vector.tensor_tensor(upper[0], upper[1], upper[2], MAX)
-            nc.scalar.copy(
-                z_w[:, run].rearrange("p (r c i t) -> p r c t i", r=2, i=4, t=PACK),
-                zs[u][:].rearrange("p (r t c i) -> p r c t i", r=2, i=4, t=PACK),
-            )
-
-        c_codes = sb("c_codes", 3 * PIECE, U32)
-        cc_codes = late.tile([P, PIECE], U32, name="cc_codes", offset=1024, align_bytes=64)
+        c_codes = sb("c_codes", V, U32)
         c_scales = sb("c_scales", V, U8)
         z_codes = sb("z_codes", V, U32)
         z_scales = sb("z_scales", V, U8)
         out_rows = out.rearrange("(m p) v -> p m v", p=P)
         res = [sb("res%d" % g, 2 * w, F32) for g, w in enumerate((256, 128, 128))]
         accs = {}
-
-        def c_piece(r):
-            return cc_codes[:] if r == 3 else c_codes[:, PIECE * r : PIECE * (r + 1)]
 
         def second_pass(r, centre, first):
             cols = slice(PIECE * r, PIECE * (r + 1))
@@ -226,14 +210,11 @@ def tile_picked_sagecat_maxrelu_e_kernel(
                     out=accs[r, m][:],
                     lhsT=w_sb[:, 2 * P * m : 2 * P * (m + 1)].bitcast(FP4X4),
                     lhsT_scale=w23_scales[:, a * N + P * m : a * N + P * (m + 1)],
-                    rhs=(c_piece(r) if centre else z_codes[:, cols]).bitcast(FP8X4),
+                    rhs=(c_codes if centre else z_codes)[:, cols].bitcast(FP8X4),
                     rhs_scale=(c_scales if centre else z_scales)[:, cols],
                     start=first,
                     stop=not first,
                 )
-
-        def quantize_c(r, values):
-            quantize(c_piece(r), c_scales[:, PIECE * r : PIECE * (r + 1)], values)
 
         def quantize_z(u):
             quantize(z_codes[:, 256 * u : 256 * (u + 1)], z_scales[:, 256 * u : 256 * (u + 1)], z_w[:, 1024 * u : 1024 * (u + 1)])
@@ -262,19 +243,40 @@ def tile_picked_sagecat_maxrelu_e_kernel(
         def store(src, lo, width):
             nc.sync.dma_start(out=out_rows[:, :, lo : lo + width], in_=src[:].rearrange("p (m v) -> p m v", m=2))
 
+        def late_low(lo, hi):
+            nc.scalar.copy(woven(mix[:, 0:1024], slice(0, 2))[:, lo:hi], by_plane(stage_b, 2)[:, lo:hi])
+
+        def late_high(g):
+            for t in (2, 3):
+                nc.vector.tensor_copy(
+                    c_late[g].rearrange("p (n t) -> p n t", t=PACK)[:, :, t],
+                    h[t][:].indirect(cen_sb[:, 16 + 8 * g : 24 + 8 * g]),
+                )
+
+        def quantize_late(g):
+            cols = slice(256 + PIECE * g, 256 + PIECE * (g + 1))
+            quantize(c_codes[:, cols], c_scales[:, cols], c_late[g])
+
+        def largest(u):
+            upper = [tile[:].rearrange("p (t v) -> p t v", t=PACK)[:, 2:PACK, 256 * u : 256 * (u + 1)] for tile in (n1, n2)]
+            nc.vector.tensor_tensor(z23[u].rearrange("p (t v) -> p t v", t=2), upper[0], upper[1], MAX)
+
+        def weave_z(u):
+            nc.scalar.copy(woven(z_w[:, 1024 * u : 1024 * (u + 1)], slice(2, PACK)), by_plane(z23[u], 2))
+
         quantize(c_codes[:, 0:256], c_scales[:, 0:256], ca_w[:])
         for r in range(2):
             second_pass(r, True, True)
         warm(3, 6, c_codes, c_scales)
-        for t in range(PACK):
-            nc.vector.tensor_copy(
-                ca[:, 512:1024].rearrange("p (u t v) -> p u t v", u=2, t=PACK)[:, :, t, :],
-                h[t][:].indirect(cen_sb[:, 16:24]),
-            )
-        cb_w = late.tile([P, 512], BF16, name="cb_w", offset=0, align_bytes=64)
-        for u in range(2):
-            weave(cb_w[:, 256 * u : 256 * (u + 1)], ca[:, 512 + 256 * u : 512 + 256 * (u + 1)])
-
+        late_low(0, 62)
+        largest(0)
+        late_high(0)
+        largest(1)
+        weave_z(0)
+        late_low(62, 64)
+        weave_z(1)
+        quantize_late(0)
+        second_pass(2, True, True)
         quantize_z(0)
         for r in range(2):
             second_pass(r, False, False)
@@ -282,18 +284,12 @@ def tile_picked_sagecat_maxrelu_e_kernel(
         for r in range(2):
             finish(r, res[0], 256, PIECE * r, ())
         store(res[0], 0, 256)
-
-        for t in range(PACK):
-            nc.vector.tensor_copy(
-                z0[:, 0:512].rearrange("p (n t) -> p n t", t=PACK)[:, :, t],
-                h[t][:].indirect(cen_sb[:, 24:32]),
-            )
+        late_high(1)
         quantize_z(1)
-        for r in (3, 2):
-            second_pass(r, False, True)
-        quantize_c(3, z0[:, 0:512])
-        quantize_c(2, cb_w[:])
-        for r in (3, 2):
-            second_pass(r, True, False)
+        second_pass(2, False, False)
+        second_pass(3, False, True)
+        quantize_late(1)
+        second_pass(3, True, False)
+        for r in (2, 3):
             finish(r, res[r - 1], 128, 0, (1,))
             store(res[r - 1], PIECE * r, 128)

@@ -149,16 +149,17 @@ def tile_picked_sagecat_maxrelu_e_kernel(
             nc.scalar.activation(h[t][:, 512:1024], acc[:], RELU)
 
         n1 = sb("n1", PACK * V, BF16)
-        n2 = sb("n2", PACK * V, BF16)
+        n2 = sb("n2", 2 * V, BF16)
         z01 = sb("z01", 2 * V, BF16)
-        mix = sb("mix", 2560, BF16)
+        mix = sb("mix", 3072, BF16)
         diff = [sb("diff0", V, F32), None]
         gain = [sb("gain%d" % t, V, F32) for t in range(2)]
         z_w = sb("z_w", PACK * V, BF16)
-        stage_a = mix[:, 496:1520]
-        stage_b = mix[:, 2032:2544]
-        z23 = (mix[:, 992:1504], mix[:, 1504:2016])
-        c_late = (mix[:, 0:512], mix[:, 512:1024])
+        n2_high = mix[:, 0:1024].rearrange("p (u t v) -> p u t v", u=2, t=2)
+        stage_a = mix[:, 1008:2032]
+        stage_b = mix[:, 2544:3056]
+        z23 = (mix[:, 1024:1536], mix[:, 512:1024])
+        c_late = (mix[:, 1504:2016], mix[:, 2016:2528])
 
         def plane(tile, t):
             return tile[:, V * t : V * (t + 1)]
@@ -169,26 +170,28 @@ def tile_picked_sagecat_maxrelu_e_kernel(
         def by_plane(src, count):
             return src.rearrange("p (t c i) -> p c t i", i=4, t=count)
 
-        for t in range(PACK):
-            if t == 3:
-                nc.vector.tensor_copy(stage_a[:, 256 * t : 256 * (t + 1)], h[t][:].indirect(cen_sb[:, 0:16]))
+        for t in range(2):
             nc.vector.tensor_copy(plane(n1, t), h[t][:].indirect(pos1_sb[:]))
             nc.vector.tensor_copy(plane(n2, t), h[t][:].indirect(pos2_sb[:]))
-            if t == 2:
-                nc.vector.tensor_copy(stage_a[:, 256 * t : 256 * (t + 1)], h[t][:].indirect(cen_sb[:, 0:16]))
-            if t < 2:
-                both = mix[:, 496:2544].rearrange("p (a v) -> p a v", v=256)[:, t : t + 7 : 6, :]
-                nc.vector.tensor_copy(both, h[t][:].indirect(cen_sb[:]))
-                if t == 1:
-                    diff[1] = sb("diff1", V, F32, tag="gain0")
-                for u in range(2):
-                    cols = slice(256 * u, 256 * (u + 1))
-                    nc.gpsimd.tensor_tensor(diff[t][:, cols], plane(n1, t)[:, cols], plane(n2, t)[:, cols], SUB)
-                    nc.scalar.activation(gain[t][:, cols], diff[t][:, cols], RELU)
-                for u in range(2):
-                    cols = slice(256 * u, 256 * (u + 1))
-                    nc.gpsimd.tensor_tensor(plane(z01, t)[:, cols], gain[t][:, cols], plane(n2, t)[:, cols], ADD)
-        nc.scalar.copy(woven(z_w[:], slice(0, 2)), by_plane(z01[:], 2))
+            both = mix[:, 1008:3056].rearrange("p (a v) -> p a v", v=256)[:, t : t + 7 : 6, :]
+            nc.vector.tensor_copy(both, h[t][:].indirect(cen_sb[:]))
+            if t == 1:
+                diff[1] = sb("diff1", V, F32, tag="gain0")
+            for u in range(2):
+                cols = slice(256 * u, 256 * (u + 1))
+                nc.gpsimd.tensor_tensor(diff[t][:, cols], plane(n1, t)[:, cols], plane(n2, t)[:, cols], SUB)
+                nc.scalar.activation(gain[t][:, cols], diff[t][:, cols], RELU)
+            for u in range(2):
+                cols = slice(256 * u, 256 * (u + 1))
+                nc.gpsimd.tensor_tensor(plane(z01, t)[:, cols], gain[t][:, cols], plane(n2, t)[:, cols], ADD)
+        for t in (2, 3):
+            nc.vector.tensor_copy(stage_a[:, 256 * t : 256 * (t + 1)], h[t][:].indirect(cen_sb[:, 0:16]))
+        nc.vector.tensor_copy(plane(n1, 2), h[2][:].indirect(pos1_sb[:]))
+        nc.vector.tensor_copy(n2_high[:, :, 0, :], h[2][:].indirect(pos2_sb[:]))
+        nc.vector.tensor_copy(plane(n1, 3), h[3][:].indirect(pos1_sb[:]))
+        nc.vector.tensor_copy(n2_high[:, 0, 1, :], h[3][:].indirect(pos2_sb[:, 0:16]))
+        for u in range(2):
+            nc.scalar.copy(woven(z_w[:], slice(0, 2))[:, 64 * u : 64 * (u + 1)], by_plane(z01[:], 2)[:, 64 * u : 64 * (u + 1)])
         ca_w = sb("ca_w", 1024, BF16, tag="z01")
         nc.scalar.copy(woven(ca_w[:], slice(0, PACK)), by_plane(stage_a, PACK))
 
@@ -244,7 +247,7 @@ def tile_picked_sagecat_maxrelu_e_kernel(
             nc.sync.dma_start(out=out_rows[:, :, lo : lo + width], in_=src[:].rearrange("p (m v) -> p m v", m=2))
 
         def late_low(lo, hi):
-            nc.scalar.copy(woven(mix[:, 0:1024], slice(0, 2))[:, lo:hi], by_plane(stage_b, 2)[:, lo:hi])
+            nc.scalar.copy(woven(mix[:, 1504:2528], slice(0, 2))[:, lo:hi], by_plane(stage_b, 2)[:, lo:hi])
 
         def late_high(g):
             for t in (2, 3):
@@ -258,8 +261,8 @@ def tile_picked_sagecat_maxrelu_e_kernel(
             quantize(c_codes[:, cols], c_scales[:, cols], c_late[g])
 
         def largest(u):
-            upper = [tile[:].rearrange("p (t v) -> p t v", t=PACK)[:, 2:PACK, 256 * u : 256 * (u + 1)] for tile in (n1, n2)]
-            nc.vector.tensor_tensor(z23[u].rearrange("p (t v) -> p t v", t=2), upper[0], upper[1], MAX)
+            first = n1[:].rearrange("p (t v) -> p t v", t=PACK)[:, 2:PACK, 256 * u : 256 * (u + 1)]
+            nc.vector.tensor_tensor(z23[u].rearrange("p (t v) -> p t v", t=2), first, n2_high[:, u], MAX)
 
         def weave_z(u):
             nc.scalar.copy(woven(z_w[:, 1024 * u : 1024 * (u + 1)], slice(2, PACK)), by_plane(z23[u], 2))
@@ -267,29 +270,29 @@ def tile_picked_sagecat_maxrelu_e_kernel(
         quantize(c_codes[:, 0:256], c_scales[:, 0:256], ca_w[:])
         for r in range(2):
             second_pass(r, True, True)
-        warm(3, 6, c_codes, c_scales)
-        late_low(0, 62)
+        warm(4, 0, c_codes, c_scales)
+        late_low(2, 64)
+        nc.vector.tensor_copy(n2_high[:, 1, 1, :], h[3][:].indirect(pos2_sb[:, 16:32]))
         largest(0)
-        late_high(0)
+        late_high(1)
         largest(1)
         weave_z(0)
-        late_low(62, 64)
+        late_low(0, 2)
         weave_z(1)
-        quantize_late(0)
-        second_pass(2, True, True)
+        quantize_late(1)
+        second_pass(3, True, True)
         quantize_z(0)
         for r in range(2):
             second_pass(r, False, False)
-        warm(2, 0, z_codes, z_scales)
         for r in range(2):
             finish(r, res[0], 256, PIECE * r, ())
         store(res[0], 0, 256)
-        late_high(1)
+        late_high(0)
         quantize_z(1)
-        second_pass(2, False, False)
-        second_pass(3, False, True)
-        quantize_late(1)
-        second_pass(3, True, False)
-        for r in (2, 3):
+        second_pass(3, False, False)
+        second_pass(2, False, True)
+        quantize_late(0)
+        second_pass(2, True, False)
+        for r in (3, 2):
             finish(r, res[r - 1], 128, 0, (1,))
             store(res[r - 1], PIECE * r, 128)

@@ -272,18 +272,18 @@ def tile_picked_sagecat_maxrelu_e_kernel(
             second_pass(r, True, True)
         warm(4, 0, c_codes, c_scales)
         late_low(2, 64)
-        nc.vector.tensor_copy(n2_high[:, 1, 1, :], h[3][:].indirect(pos2_sb[:, 16:32]))
         largest(0)
+        nc.vector.tensor_copy(n2_high[:, 1, 1, :], h[3][:].indirect(pos2_sb[:, 16:32]))
         late_high(1)
         largest(1)
         weave_z(0)
         late_low(0, 2)
         weave_z(1)
-        quantize_late(1)
-        second_pass(3, True, True)
         quantize_z(0)
         for r in range(2):
             second_pass(r, False, False)
+        quantize_late(1)
+        second_pass(3, True, True)
         for r in range(2):
             finish(r, res[0], 256, PIECE * r, ())
         store(res[0], 0, 256)

@@ -151,15 +151,16 @@ def tile_picked_sagecat_maxrelu_e_kernel(
         n1 = sb("n1", PACK * V, BF16)
         n2 = sb("n2", 2 * V, BF16)
         z01 = sb("z01", 2 * V, BF16)
-        mix = sb("mix", 3072, BF16)
+        mix = sb("mix", 3328, BF16)
         diff = [sb("diff0", V, F32), None]
         gain = [sb("gain%d" % t, V, F32) for t in range(2)]
         z_w = sb("z_w", PACK * V, BF16)
-        n2_high = mix[:, 0:1024].rearrange("p (u t v) -> p u t v", u=2, t=2)
+        n2_high = mix[:, 0:1024].rearrange("p (g t v) -> p g t v", g=4, t=2)
         stage_a = mix[:, 1008:2032]
-        stage_b = mix[:, 2544:3056]
-        z23 = (mix[:, 1024:1536], mix[:, 512:1024])
-        c_late = (mix[:, 1504:2016], mix[:, 2016:2528])
+        stage_b = mix[:, 2800:3312]
+        z23 = (mix[:, 2016:2784], mix[:, 768:1024])
+        c_late = (mix[:, 1024:1536], mix[:, 1536:2048])
+        z_groups = (slice(0, 3), slice(3, 4))
 
         def plane(tile, t):
             return tile[:, V * t : V * (t + 1)]
@@ -173,7 +174,7 @@ def tile_picked_sagecat_maxrelu_e_kernel(
         for t in range(2):
             nc.vector.tensor_copy(plane(n1, t), h[t][:].indirect(pos1_sb[:]))
             nc.vector.tensor_copy(plane(n2, t), h[t][:].indirect(pos2_sb[:]))
-            both = mix[:, 1008:3056].rearrange("p (a v) -> p a v", v=256)[:, t : t + 7 : 6, :]
+            both = mix[:, 1008:3312].rearrange("p (a v) -> p a v", v=256)[:, t : t + 8 : 7, :]
             nc.vector.tensor_copy(both, h[t][:].indirect(cen_sb[:]))
             if t == 1:
                 diff[1] = sb("diff1", V, F32, tag="gain0")
@@ -189,7 +190,7 @@ def tile_picked_sagecat_maxrelu_e_kernel(
         nc.vector.tensor_copy(plane(n1, 2), h[2][:].indirect(pos1_sb[:]))
         nc.vector.tensor_copy(n2_high[:, :, 0, :], h[2][:].indirect(pos2_sb[:]))
         nc.vector.tensor_copy(plane(n1, 3), h[3][:].indirect(pos1_sb[:]))
-        nc.vector.tensor_copy(n2_high[:, 0, 1, :], h[3][:].indirect(pos2_sb[:, 0:16]))
+        nc.vector.tensor_copy(n2_high[:, 0:3, 1, :], h[3][:].indirect(pos2_sb[:, 0:24]))
         for u in range(2):
             nc.scalar.copy(woven(z_w[:], slice(0, 2))[:, 64 * u : 64 * (u + 1)], by_plane(z01[:], 2)[:, 64 * u : 64 * (u + 1)])
         ca_w = sb("ca_w", 1024, BF16, tag="z01")
@@ -219,8 +220,8 @@ def tile_picked_sagecat_maxrelu_e_kernel(
                     stop=not first,
                 )
 
-        def quantize_z(u):
-            quantize(z_codes[:, 256 * u : 256 * (u + 1)], z_scales[:, 256 * u : 256 * (u + 1)], z_w[:, 1024 * u : 1024 * (u + 1)])
+        def quantize_z(lo, hi):
+            quantize(z_codes[:, lo:hi], z_scales[:, lo:hi], z_w[:, PACK * lo : PACK * hi])
 
         def finish(r, dst, width, lo, vector_ms):
             for m in range(2):
@@ -247,7 +248,7 @@ def tile_picked_sagecat_maxrelu_e_kernel(
             nc.sync.dma_start(out=out_rows[:, :, lo : lo + width], in_=src[:].rearrange("p (m v) -> p m v", m=2))
 
         def late_low(lo, hi):
-            nc.scalar.copy(woven(mix[:, 1504:2528], slice(0, 2))[:, lo:hi], by_plane(stage_b, 2)[:, lo:hi])
+            nc.scalar.copy(woven(mix[:, 1024:2048], slice(0, 2))[:, lo:hi], by_plane(stage_b, 2)[:, lo:hi])
 
         def late_high(g):
             for t in (2, 3):
@@ -261,38 +262,45 @@ def tile_picked_sagecat_maxrelu_e_kernel(
             quantize(c_codes[:, cols], c_scales[:, cols], c_late[g])
 
         def largest(u):
-            first = n1[:].rearrange("p (t v) -> p t v", t=PACK)[:, 2:PACK, 256 * u : 256 * (u + 1)]
-            nc.vector.tensor_tensor(z23[u].rearrange("p (t v) -> p t v", t=2), first, n2_high[:, u], MAX)
+            first = n1[:].rearrange("p (t g v) -> p g t v", t=PACK, g=4)[:, z_groups[u], 2:PACK, :]
+            nc.vector.tensor_tensor(z23[u].rearrange("p (g t v) -> p g t v", t=2, v=PIECE), first, n2_high[:, z_groups[u]], MAX)
 
-        def weave_z(u):
-            nc.scalar.copy(woven(z_w[:, 1024 * u : 1024 * (u + 1)], slice(2, PACK)), by_plane(z23[u], 2))
+        def weave_z(u, lo, hi):
+            first = z_groups[u].start
+            nc.scalar.copy(
+                z_w[:].rearrange("p (g c i t) -> p g c t i", g=4, i=4, t=PACK)[:, first + lo : first + hi, :, 2:PACK, :],
+                z23[u].rearrange("p (g t c i) -> p g c t i", t=2, c=PIECE // 4, i=4)[:, lo:hi],
+            )
 
         quantize(c_codes[:, 0:256], c_scales[:, 0:256], ca_w[:])
         for r in range(2):
             second_pass(r, True, True)
         warm(4, 0, c_codes, c_scales)
-        late_low(2, 64)
+        late_low(0, 62)
         largest(0)
-        nc.vector.tensor_copy(n2_high[:, 1, 1, :], h[3][:].indirect(pos2_sb[:, 16:32]))
-        late_high(1)
+        nc.vector.tensor_copy(n2_high[:, 3, 1, :], h[3][:].indirect(pos2_sb[:, 24:32]))
+        late_high(0)
         largest(1)
-        weave_z(0)
-        late_low(0, 2)
-        weave_z(1)
-        quantize_z(0)
+        weave_z(0, 0, 2)
+        weave_z(0, 2, 3)
+        late_low(62, 64)
+        weave_z(1, 0, 1)
+        quantize_late(0)
+        second_pass(2, True, True)
+        quantize_z(0, 256)
         for r in range(2):
             second_pass(r, False, False)
-        quantize_late(1)
-        second_pass(3, True, True)
+        quantize_z(256, 384)
+        second_pass(2, False, False)
         for r in range(2):
             finish(r, res[0], 256, PIECE * r, ())
         store(res[0], 0, 256)
-        late_high(0)
-        quantize_z(1)
-        second_pass(3, False, False)
-        second_pass(2, False, True)
-        quantize_late(0)
-        second_pass(2, True, False)
-        for r in (3, 2):
-            finish(r, res[r - 1], 128, 0, (1,))
-            store(res[r - 1], PIECE * r, 128)
+        finish(2, res[1], 128, 0, ())
+        store(res[1], PIECE * 2, 128)
+        late_high(1)
+        quantize_z(384, 512)
+        second_pass(3, False, True)
+        quantize_late(1)
+        second_pass(3, True, False)
+        finish(3, res[2], 128, 0, (1,))
+        store(res[2], PIECE * 3, 128)

@@ -231,15 +231,15 @@ def tile_picked_sagecat_maxrelu_e_kernel(
                 else:
                     nc.scalar.activation(cols, accs[r, m][:], RELU)
 
-        def warm(count, first_bank, codes, scales):
+        def warm(count):
             for i in range(count):
-                spare = bank(first_bank + i % 2, "spare%d_%d" % (first_bank, i), 256)
+                spare = bank(i, "spare%d" % i, 512)
                 nc.tensor.matmul_mx(
                     out=spare[:],
-                    lhsT=w1_codes[:, 0:P].bitcast(FP8X4),
-                    lhsT_scale=w1_scales[:, 0:P],
-                    rhs=codes[:, 0:256].bitcast(FP8X4),
-                    rhs_scale=scales[:, 0:256],
+                    lhsT=c_codes[:, 0:P].bitcast(FP8X4),
+                    lhsT_scale=c_scales[:, 0:P],
+                    rhs=x_codes(512, 1024).bitcast(FP8X4),
+                    rhs_scale=x_scales[:, 512:1024],
                     start=True,
                     stop=True,
                 )
@@ -275,7 +275,7 @@ def tile_picked_sagecat_maxrelu_e_kernel(
         quantize(c_codes[:, 0:256], c_scales[:, 0:256], ca_w[:])
         for r in range(2):
             second_pass(r, True, True)
-        warm(4, 0, c_codes, c_scales)
+        warm(2)
         late_low(0, 62)
         largest(0)
         nc.vector.tensor_copy(n2_high[:, 3, 1, :], h[3][:].indirect(pos2_sb[:, 24:32]))

@@ -89,10 +89,10 @@ def tile_picked_sagecat_maxrelu_e_kernel(
             raw = w1_raw[u][:].rearrange("p (j m t) -> p m j t", j=PACK, t=PACK)
             nc.scalar.copy(dealt[:, :, :, ts], raw[:, :, :, ts])
 
-        deal_w1(0, 0)
+        deal_w1(0, slice(0, 2))
         deal_w1(1, 0)
         deal_w1(2, slice(0, PACK))
-        deal_w1(0, slice(1, PACK))
+        deal_w1(0, slice(2, PACK))
         deal_w1(1, slice(1, PACK))
 
         xa_codes = sb("xa_codes", 256, U32)
@@ -135,7 +135,7 @@ def tile_picked_sagecat_maxrelu_e_kernel(
         for r, (lo, hi) in enumerate(x_runs):
             acc = bank(r, "acc_h0_%d" % r, hi - lo)
             product(acc[:], 0, lo, hi)
-            if r == 2:
+            if r == 3:
                 nc.vector.tensor_scalar_max(h[0][:, lo:hi], acc[:], 0.0)
             else:
                 nc.scalar.activation(h[0][:, lo:hi], acc[:], RELU)

@@ -17,6 +17,7 @@ RELU = mybir.ActivationFunctionType.Relu
 MAX = mybir.AluOpType.max
 ADD = mybir.AluOpType.add
 SUB = mybir.AluOpType.subtract
+MULT = mybir.AluOpType.mult
 
 P = 128
 PACK = 4
@@ -50,14 +51,10 @@ def tile_picked_sagecat_maxrelu_e_kernel(
         nc.sync.dma_start(offs_sb[:], offs)
         for j in range(1, PACK):
             nc.sync.dma_start(out=x_sb[j][:], in_=x_rows[:, j, :])
-        w1_rows = w1.rearrange("(p j) c -> p j c", j=PACK)
-        w1_cuts = (0, 320, 480, 512)
-        w1_raw = [sb("w1_raw%d" % u, PACK * (w1_cuts[u + 1] - w1_cuts[u]), F32) for u in range(3)]
-        for u in range(3):
-            nc.sync.dma_start(
-                out=w1_raw[u][:].rearrange("p (j c) -> p j c", j=PACK),
-                in_=w1_rows[:, :, w1_cuts[u] : w1_cuts[u + 1]],
-            )
+        w1_rows = w1.rearrange("(p j) c -> p (j c)", j=PACK)
+        w1_raw = [sb("w1_raw%d" % u, 2 * H, F32) for u in range(2)]
+        for u in range(2):
+            nc.sync.dma_start(out=w1_raw[u][:], in_=w1_rows[:, 2 * H * u : 2 * H * (u + 1)])
         nc.sync.dma_start(pos1_sb[:], pos1)
         nc.sync.dma_start(pos2_sb[:], pos2)
         nc.sync.dma_start(cen_sb[:], cen)
@@ -84,19 +81,18 @@ def tile_picked_sagecat_maxrelu_e_kernel(
                 )
 
         w1_bf = sb("w1_bf", PACK * H, BF16)
-        def deal_w1(u, ts):
-            dealt = w1_bf[:].rearrange("p (t m j) -> p m j t", t=PACK, j=PACK)[:, w1_cuts[u] // PACK : w1_cuts[u + 1] // PACK]
-            raw = w1_raw[u][:].rearrange("p (j m t) -> p m j t", j=PACK, t=PACK)
-            nc.scalar.copy(dealt[:, :, :, ts], raw[:, :, :, ts])
 
-        deal_w1(0, slice(0, 2))
-        deal_w1(1, 0)
-        deal_w1(2, slice(0, PACK))
-        deal_w1(0, slice(2, PACK))
-        deal_w1(1, slice(1, PACK))
+        def deal_views(u, ts):
+            dealt = w1_bf[:].rearrange("p (t m j) -> p m t j", t=PACK, j=PACK)[:, :, ts, 2 * u : 2 * u + 2]
+            raw = w1_raw[u][:].rearrange("p (j m t) -> p m t j", j=2, t=PACK)[:, :, ts, :]
+            return dealt, raw
 
-        xa_codes = sb("xa_codes", 256, U32)
-        xb_codes = sb("xb_codes", 768, U32, tag="w1_raw2")
+        nc.scalar.copy(*deal_views(0, slice(0, 2)))
+        nc.gpsimd.tensor_scalar(*deal_views(0, slice(2, 4)), 1.0, 0.0, MULT, ADD)
+        nc.vector.tensor_copy(*deal_views(1, 0))
+        nc.scalar.copy(*deal_views(1, slice(1, 4)))
+
+        x_all_codes = sb("x_all_codes", S, U32, tag="w1_raw0")
         x_scales = sb("x_scales", S, U8)
         w1_codes = sb("w1_codes", H, U32)
         w1_scales = sb("w1_scales", H, U8)
@@ -105,7 +101,7 @@ def tile_picked_sagecat_maxrelu_e_kernel(
             quantize(w1_codes[:, lo:hi], w1_scales[:, lo:hi], w1_bf[:, PACK * lo : PACK * hi])
 
         def x_codes(lo, hi):
-            return xa_codes[:, lo:hi] if hi <= 256 else xb_codes[:, lo - 256 : hi - 256]
+            return x_all_codes[:, lo:hi]
 
         def quantize_x(lo, hi):
             quantize(x_codes(lo, hi), x_scales[:, lo:hi], xg[lo // half][:, PACK * (lo % half) : PACK * (lo % half + hi - lo)])

@@ -22,6 +22,7 @@ MULT = mybir.AluOpType.mult
 P = 128
 PACK = 4
 PIECE = 128
+LATE = 384
 
 
 def tile_picked_sagecat_maxrelu_e_kernel(
@@ -51,10 +52,11 @@ def tile_picked_sagecat_maxrelu_e_kernel(
         nc.sync.dma_start(offs_sb[:], offs)
         for j in range(1, PACK):
             nc.sync.dma_start(out=x_sb[j][:], in_=x_rows[:, j, :])
-        w1_rows = w1.rearrange("(p j) c -> p (j c)", j=PACK)
-        w1_raw = [sb("w1_raw%d" % u, 2 * H, F32) for u in range(2)]
-        for u in range(2):
-            nc.sync.dma_start(out=w1_raw[u][:], in_=w1_rows[:, 2 * H * u : 2 * H * (u + 1)])
+        w1_rows = w1.rearrange("(p j) c -> p j c", j=PACK)
+        w1_parts = ((0, 0, H), (2, 0, LATE), (2, LATE, H))
+        w1_raw = [sb("w1_raw%d" % u, 2 * (hi - lo), F32) for u, (j, lo, hi) in enumerate(w1_parts)]
+        for u, (j, lo, hi) in enumerate(w1_parts):
+            nc.sync.dma_start(out=w1_raw[u][:].rearrange("p (j c) -> p j c", j=2), in_=w1_rows[:, j : j + 2, lo:hi])
         nc.sync.dma_start(pos1_sb[:], pos1)
         nc.sync.dma_start(pos2_sb[:], pos2)
         nc.sync.dma_start(cen_sb[:], cen)
@@ -83,16 +85,19 @@ def tile_picked_sagecat_maxrelu_e_kernel(
         w1_bf = sb("w1_bf", PACK * H, BF16)
 
         def deal_views(u, ts):
-            dealt = w1_bf[:].rearrange("p (t m j) -> p m t j", t=PACK, j=PACK)[:, :, ts, 2 * u : 2 * u + 2]
+            j, lo, hi = w1_parts[u]
+            dealt = w1_bf[:].rearrange("p (t m j) -> p m t j", t=PACK, j=PACK)[:, lo // PACK : hi // PACK, ts, j : j + 2]
             raw = w1_raw[u][:].rearrange("p (j m t) -> p m t j", j=2, t=PACK)[:, :, ts, :]
             return dealt, raw
 
-        nc.scalar.copy(*deal_views(0, slice(0, 2)))
-        nc.gpsimd.tensor_scalar(*deal_views(0, slice(2, 4)), 1.0, 0.0, MULT, ADD)
-        nc.vector.tensor_copy(*deal_views(1, 0))
+        nc.scalar.copy(*deal_views(0, 0))
+        nc.gpsimd.tensor_scalar(*deal_views(0, slice(1, 4)), 1.0, 0.0, MULT, ADD)
+        nc.scalar.copy(*deal_views(1, 0))
+        nc.scalar.copy(*deal_views(2, slice(0, 4)))
         nc.scalar.copy(*deal_views(1, slice(1, 4)))
 
-        x_all_codes = sb("x_all_codes", S, U32, tag="w1_raw0")
+        xa_codes = sb("xa_codes", 256, U32)
+        xb_codes = sb("xb_codes", 768, U32, tag="w1_raw2")
         x_scales = sb("x_scales", S, U8)
         w1_codes = sb("w1_codes", H, U32)
         w1_scales = sb("w1_scales", H, U8)
@@ -101,7 +106,7 @@ def tile_picked_sagecat_maxrelu_e_kernel(
             quantize(w1_codes[:, lo:hi], w1_scales[:, lo:hi], w1_bf[:, PACK * lo : PACK * hi])
 
         def x_codes(lo, hi):
-            return x_all_codes[:, lo:hi]
+            return xa_codes[:, lo:hi] if hi <= 256 else xb_codes[:, lo - 256 : hi - 256]
 
         def quantize_x(lo, hi):
             quantize(x_codes(lo, hi), x_scales[:, lo:hi], xg[lo // half][:, PACK * (lo % half) : PACK * (lo % half + hi - lo)])

@@ -149,34 +149,37 @@ def tile_picked_sagecat_maxrelu_e_kernel(
             product(acc[:], t, 512, 1024)
             nc.scalar.activation(h[t][:, 512:1024], acc[:], RELU)
 
-        n1 = sb("n1", PACK * V, BF16)
+        n1 = sb("n1", 2 * V, BF16)
         n2 = sb("n2", 2 * V, BF16)
-        z01 = sb("z01", 2 * V, BF16)
-        mix = sb("mix", 3328, BF16)
+        n1_high = sb("n1_high", 2 * V, BF16)
+        mix = sb("mix", 7168, BF16)
         diff = [sb("diff0", V, F32), None]
         gain = [sb("gain%d" % t, V, F32) for t in range(2)]
         z_w = sb("z_w", PACK * V, BF16)
-        n2_high = mix[:, 0:1024].rearrange("p (g t v) -> p g t v", g=4, t=2)
-        stage_a = mix[:, 1008:2032]
-        stage_b = mix[:, 2800:3312]
-        z23 = (mix[:, 2016:2784], mix[:, 768:1024])
-        c_late = (mix[:, 1024:1536], mix[:, 1536:2048])
-        z_groups = (slice(0, 3), slice(3, 4))
+        C_LOW, Z_LOW, Z_HIGH, C_EARLY, N2_LAST, C_LAST, C_THIRD = 0, 1792, 2816, 3568, 3840, 1024, 1534
+        n2_high = sb("n2_high", 2 * 384, BF16)
+        c_last = mix[:, C_LAST : C_LAST + PACK * PIECE]
 
         def plane(tile, t):
             return tile[:, V * t : V * (t + 1)]
 
-        def woven(dst, planes):
-            return dst.rearrange("p (c i t) -> p c t i", i=4, t=PACK)[:, :, planes, :]
+        def slot(pairs, e):
+            return pairs.rearrange("p (v e) -> p v e", e=2)[:, :, e]
 
-        def by_plane(src, count):
-            return src.rearrange("p (t c i) -> p c t i", i=4, t=count)
+        def region(start, lo, hi):
+            return mix[:, start + 2 * lo : start + 2 * hi]
+
+        def weave(dst, low, high, count):
+            both = mix[:, low : low + 2 * (high - low)].bitcast(U32).rearrange("p (u x) -> p u x", u=2)[:, :, 0:count]
+            nc.scalar.copy(
+                dst.bitcast(U32).rearrange("p (c i u) -> p c u i", i=2, u=2),
+                both.rearrange("p u (c i) -> p c u i", i=2),
+            )
 
         for t in range(2):
             nc.vector.tensor_copy(plane(n1, t), h[t][:].indirect(pos1_sb[:]))
             nc.vector.tensor_copy(plane(n2, t), h[t][:].indirect(pos2_sb[:]))
-            both = mix[:, 1008:3312].rearrange("p (a v) -> p a v", v=256)[:, t : t + 8 : 7, :]
-            nc.vector.tensor_copy(both, h[t][:].indirect(cen_sb[:]))
+            nc.vector.tensor_copy(slot(region(C_LOW, 0, V), t), h[t][:].indirect(cen_sb[:]))
             if t == 1:
                 diff[1] = sb("diff1", V, F32, tag="gain0")
             for u in range(2):
@@ -185,17 +188,19 @@ def tile_picked_sagecat_maxrelu_e_kernel(
                 nc.scalar.activation(gain[t][:, cols], diff[t][:, cols], RELU)
             for u in range(2):
                 cols = slice(256 * u, 256 * (u + 1))
-                nc.gpsimd.tensor_tensor(plane(z01, t)[:, cols], gain[t][:, cols], plane(n2, t)[:, cols], ADD)
+                nc.gpsimd.tensor_tensor(slot(region(Z_LOW, 0, V), t)[:, cols], gain[t][:, cols], plane(n2, t)[:, cols], ADD)
         for t in (2, 3):
-            nc.vector.tensor_copy(stage_a[:, 256 * t : 256 * (t + 1)], h[t][:].indirect(cen_sb[:, 0:16]))
-        nc.vector.tensor_copy(plane(n1, 2), h[2][:].indirect(pos1_sb[:]))
-        nc.vector.tensor_copy(n2_high[:, :, 0, :], h[2][:].indirect(pos2_sb[:]))
-        nc.vector.tensor_copy(plane(n1, 3), h[3][:].indirect(pos1_sb[:]))
-        nc.vector.tensor_copy(n2_high[:, 0:3, 1, :], h[3][:].indirect(pos2_sb[:, 0:24]))
-        for u in range(2):
-            nc.scalar.copy(woven(z_w[:], slice(0, 2))[:, 64 * u : 64 * (u + 1)], by_plane(z01[:], 2)[:, 64 * u : 64 * (u + 1)])
-        ca_w = sb("ca_w", 1024, BF16, tag="z01")
-        nc.scalar.copy(woven(ca_w[:], slice(0, PACK)), by_plane(stage_a, PACK))
+            nc.vector.tensor_copy(slot(region(C_EARLY, 0, 256), t - 2), h[t][:].indirect(cen_sb[:, 0:16]))
+        for t in (2, 3):
+            nc.vector.tensor_copy(slot(n1_high[:], t - 2), h[t][:].indirect(pos1_sb[:]))
+            nc.vector.tensor_copy(slot(n2_high[:], t - 2), h[t][:].indirect(pos2_sb[:, 0:24]))
+        ca_w = sb("ca_w", 1024, BF16, tag="gain1")
+        weave(ca_w[:], C_LOW, C_EARLY, 256)
+        nc.scalar.copy(
+            c_last.bitcast(U32).rearrange("p (v u) -> p v u", u=2)[:, :, 0],
+            region(C_LOW, 384, V).bitcast(U32),
+        )
+        cb_w = sb("cb_w", PACK * PIECE, BF16)
 
         c_codes = sb("c_codes", V, U32)
         c_scales = sb("c_scales", V, U8)
@@ -248,60 +253,46 @@ def tile_picked_sagecat_maxrelu_e_kernel(
         def store(src, lo, width):
             nc.sync.dma_start(out=out_rows[:, :, lo : lo + width], in_=src[:].rearrange("p (m v) -> p m v", m=2))
 
-        def late_low(lo, hi):
-            nc.scalar.copy(woven(mix[:, 1024:2048], slice(0, 2))[:, lo:hi], by_plane(stage_b, 2)[:, lo:hi])
+        def quantize_c(lo, hi, values):
+            quantize(c_codes[:, lo:hi], c_scales[:, lo:hi], values)
 
-        def late_high(g):
-            for t in (2, 3):
-                nc.vector.tensor_copy(
-                    c_late[g].rearrange("p (n t) -> p n t", t=PACK)[:, :, t],
-                    h[t][:].indirect(cen_sb[:, 16 + 8 * g : 24 + 8 * g]),
-                )
+        def largest(lo, hi, second):
+            nc.vector.tensor_tensor(region(Z_HIGH, lo, hi), n1_high[:, 2 * lo : 2 * hi], second, MAX)
 
-        def quantize_late(g):
-            cols = slice(256 + PIECE * g, 256 + PIECE * (g + 1))
-            quantize(c_codes[:, cols], c_scales[:, cols], c_late[g])
+        def weave_z(lo, hi):
+            weave(z_w[:, PACK * lo : PACK * hi], Z_LOW + 2 * lo, Z_HIGH + 2 * lo, hi - lo)
 
-        def largest(u):
-            first = n1[:].rearrange("p (t g v) -> p g t v", t=PACK, g=4)[:, z_groups[u], 2:PACK, :]
-            nc.vector.tensor_tensor(z23[u].rearrange("p (g t v) -> p g t v", t=2, v=PIECE), first, n2_high[:, z_groups[u]], MAX)
-
-        def weave_z(u, lo, hi):
-            first = z_groups[u].start
-            nc.scalar.copy(
-                z_w[:].rearrange("p (g c i t) -> p g c t i", g=4, i=4, t=PACK)[:, first + lo : first + hi, :, 2:PACK, :],
-                z23[u].rearrange("p (g t c i) -> p g c t i", t=2, c=PIECE // 4, i=4)[:, lo:hi],
-            )
-
-        quantize(c_codes[:, 0:256], c_scales[:, 0:256], ca_w[:])
+        quantize_c(0, 256, ca_w[:])
         for r in range(2):
             second_pass(r, True, True)
         warm(2)
-        late_low(0, 62)
-        largest(0)
-        nc.vector.tensor_copy(n2_high[:, 3, 1, :], h[3][:].indirect(pos2_sb[:, 24:32]))
-        late_high(0)
-        largest(1)
-        weave_z(0, 0, 2)
-        weave_z(0, 2, 3)
-        late_low(62, 64)
-        weave_z(1, 0, 1)
-        quantize_late(0)
-        second_pass(2, True, True)
+        largest(0, 384, n2_high[:])
+        for t in (2, 3):
+            nc.vector.tensor_copy(slot(region(N2_LAST, 0, PIECE), t - 2), h[t][:].indirect(pos2_sb[:, 24:32]))
+        for t in (2, 3):
+            nc.vector.tensor_copy(slot(region(C_THIRD, 0, PIECE), t - 2), h[t][:].indirect(cen_sb[:, 16:24]))
+        largest(384, V, region(N2_LAST, 0, PIECE))
+        weave_z(0, 256)
+        weave_z(256, 384)
+        weave(cb_w[:], C_LOW + 512, C_THIRD, PIECE)
+        weave_z(384, V)
         quantize_z(0, 256)
         for r in range(2):
             second_pass(r, False, False)
         quantize_z(256, 384)
-        second_pass(2, False, False)
+        second_pass(2, False, True)
+        quantize_c(256, 384, cb_w[:])
+        second_pass(2, True, False)
         for r in range(2):
             finish(r, res[0], 256, PIECE * r, ())
         store(res[0], 0, 256)
         finish(2, res[1], 128, 0, ())
         store(res[1], PIECE * 2, 128)
-        late_high(1)
+        for t in (2, 3):
+            nc.vector.tensor_copy(c_last.rearrange("p (n t) -> p n t", t=PACK)[:, :, t], h[t][:].indirect(cen_sb[:, 24:32]))
         quantize_z(384, 512)
         second_pass(3, False, True)
-        quantize_late(1)
+        quantize_c(384, V, c_last)
         second_pass(3, True, False)
         finish(3, res[2], 128, 0, (1,))
         store(res[2], PIECE * 3, 128)

@@ -14,14 +14,13 @@ U8 = mybir.dt.uint8
 FP8X4 = mybir.dt.float8_e4m3fn_x4
 FP4X4 = mybir.dt.float4_e2m1fn_x4
 RELU = mybir.ActivationFunctionType.Relu
+COPY = mybir.ActivationFunctionType.Copy
 MAX = mybir.AluOpType.max
 ADD = mybir.AluOpType.add
-SUB = mybir.AluOpType.subtract
 MULT = mybir.AluOpType.mult
 
 P = 128
 PACK = 4
-PIECE = 128
 LATE = 384
 
 
@@ -149,150 +148,82 @@ def tile_picked_sagecat_maxrelu_e_kernel(
             product(acc[:], t, 512, 1024)
             nc.scalar.activation(h[t][:, 512:1024], acc[:], RELU)
 
-        n1 = sb("n1", 2 * V, BF16)
-        n2 = sb("n2", 2 * V, BF16)
-        n1_high = sb("n1_high", 2 * V, BF16)
-        mix = sb("mix", 7168, BF16)
-        diff = [sb("diff0", V, F32), None]
-        gain = [sb("gain%d" % t, V, F32) for t in range(2)]
-        z_w = sb("z_w", PACK * V, BF16)
-        C_LOW, Z_LOW, Z_HIGH, C_EARLY, N2_LAST, C_LAST, C_THIRD = 0, 1792, 2816, 3568, 3840, 1024, 1534
-        n2_high = sb("n2_high", 2 * 384, BF16)
-        c_last = mix[:, C_LAST : C_LAST + PACK * PIECE]
+        groups = ((0, 256), (256, 384), (384, 512))
+        low = [sb("n%d_low" % d, 2 * V, BF16) for d in range(2)]
+        high = [[sb("n%d_high%d" % (d, g), 2 * (hi - lo), BF16) for g, (lo, hi) in enumerate(groups)] for d in range(2)]
+        c_pairs = sb("c_pairs", PACK * V, BF16)
+        c_w = sb("c_w", PACK * V, BF16)
+        z_planes = sb("z_planes", PACK * V, BF16)
+        z_w = [sb("z_w%d" % g, PACK * (hi - lo), BF16) for g, (lo, hi) in enumerate(groups)]
+        lists = (pos1_sb, pos2_sb)
 
-        def plane(tile, t):
-            return tile[:, V * t : V * (t + 1)]
-
-        def slot(pairs, e):
-            return pairs.rearrange("p (v e) -> p v e", e=2)[:, :, e]
-
-        def region(start, lo, hi):
-            return mix[:, start + 2 * lo : start + 2 * hi]
-
-        def weave(dst, low, high, count):
-            both = mix[:, low : low + 2 * (high - low)].bitcast(U32).rearrange("p (u x) -> p u x", u=2)[:, :, 0:count]
-            nc.scalar.copy(
-                dst.bitcast(U32).rearrange("p (c i u) -> p c u i", i=2, u=2),
-                both.rearrange("p u (c i) -> p c u i", i=2),
-            )
-
-        for t in range(2):
-            nc.vector.tensor_copy(plane(n1, t), h[t][:].indirect(pos1_sb[:]))
-            nc.vector.tensor_copy(plane(n2, t), h[t][:].indirect(pos2_sb[:]))
-            nc.vector.tensor_copy(slot(region(C_LOW, 0, V), t), h[t][:].indirect(cen_sb[:]))
-            if t == 1:
-                diff[1] = sb("diff1", V, F32, tag="gain0")
-            for u in range(2):
-                cols = slice(256 * u, 256 * (u + 1))
-                nc.gpsimd.tensor_tensor(diff[t][:, cols], plane(n1, t)[:, cols], plane(n2, t)[:, cols], SUB)
-                nc.scalar.activation(gain[t][:, cols], diff[t][:, cols], RELU)
-            for u in range(2):
-                cols = slice(256 * u, 256 * (u + 1))
-                nc.gpsimd.tensor_tensor(slot(region(Z_LOW, 0, V), t)[:, cols], gain[t][:, cols], plane(n2, t)[:, cols], ADD)
-        for t in (2, 3):
-            nc.vector.tensor_copy(slot(region(C_EARLY, 0, 256), t - 2), h[t][:].indirect(cen_sb[:, 0:16]))
-        for t in (2, 3):
-            nc.vector.tensor_copy(slot(n1_high[:], t - 2), h[t][:].indirect(pos1_sb[:]))
-            nc.vector.tensor_copy(slot(n2_high[:], t - 2), h[t][:].indirect(pos2_sb[:, 0:24]))
-        ca_w = sb("ca_w", 1024, BF16, tag="gain1")
-        weave(ca_w[:], C_LOW, C_EARLY, 256)
-        nc.scalar.copy(
-            c_last.bitcast(U32).rearrange("p (v u) -> p v u", u=2)[:, :, 0],
-            region(C_LOW, 384, V).bitcast(U32),
-        )
-        cb_w = sb("cb_w", PACK * PIECE, BF16)
+        for d in range(2):
+            nc.vector.tensor_copy(low[d][:, 0:V], h[0][:].indirect(lists[d][:]))
+        for t in range(PACK):
+            pair = c_pairs[:, 2 * V * (t // 2) : 2 * V * (t // 2 + 1)].rearrange("p (v e) -> p v e", e=2)
+            nc.vector.tensor_copy(pair[:, :, t % 2], h[t][:].indirect(cen_sb[:]))
+        for d in range(2):
+            nc.scalar.activation(low[d][:, V : 2 * V], h[1][:].indirect(lists[d][:]), COPY)
+        for g, (lo, hi) in enumerate(groups):
+            w = hi - lo
+            for t in (2, 3):
+                for d in range(2):
+                    nc.scalar.activation(
+                        high[d][g][:, w * (t - 2) : w * (t - 1)], h[t][:].indirect(lists[d][:, lo // 16 : hi // 16]), COPY
+                    )
 
         c_codes = sb("c_codes", V, U32)
         c_scales = sb("c_scales", V, U8)
         z_codes = sb("z_codes", V, U32)
         z_scales = sb("z_scales", V, U8)
         out_rows = out.rearrange("(m p) v -> p m v", p=P)
-        res = [sb("res%d" % g, 2 * w, F32) for g, w in enumerate((256, 128, 128))]
         accs = {}
 
-        def second_pass(r, centre, first):
-            cols = slice(PIECE * r, PIECE * (r + 1))
+        def second_pass(g, centre):
+            lo, hi = groups[g]
             w_sb, a = (w2_sb, 1) if centre else (w3_sb, 0)
             for m in range(2):
-                if first:
-                    accs[r, m] = bank((2 * r + m + 2) % 8, "acc_o%d_%d" % (r, m), PIECE)
+                if centre:
+                    accs[g, m] = bank((2 * g + m + 2) % 8, "acc_o%d_%d" % (g, m), hi - lo)
                 nc.tensor.matmul_mx(
-                    out=accs[r, m][:],
+                    out=accs[g, m][:],
                     lhsT=w_sb[:, 2 * P * m : 2 * P * (m + 1)].bitcast(FP4X4),
                     lhsT_scale=w23_scales[:, a * N + P * m : a * N + P * (m + 1)],
-                    rhs=(c_codes if centre else z_codes)[:, cols].bitcast(FP8X4),
-                    rhs_scale=(c_scales if centre else z_scales)[:, cols],
-                    start=first,
-                    stop=not first,
+                    rhs=(c_codes if centre else z_codes)[:, lo:hi].bitcast(FP8X4),
+                    rhs_scale=(c_scales if centre else z_scales)[:, lo:hi],
+                    start=centre,
+                    stop=not centre,
                 )
 
-        def quantize_z(lo, hi):
-            quantize(z_codes[:, lo:hi], z_scales[:, lo:hi], z_w[:, PACK * lo : PACK * hi])
-
-        def finish(r, dst, width, lo, vector_ms):
+        nc.vector.tensor_copy(
+            c_w[:].bitcast(I32).rearrange("p (c i u) -> p c u i", i=4, u=2),
+            c_pairs[:].bitcast(I32).rearrange("p (u c i) -> p c u i", i=4, u=2),
+        )
+        nc.vector.tensor_tensor(z_planes[:, 0 : 2 * V], low[0][:], low[1][:], MAX)
+        quantize(c_codes[:], c_scales[:], c_w[:])
+        for g in range(len(groups)):
+            second_pass(g, True)
+        z_view = z_planes[:].rearrange("p (t v) -> p t v", t=PACK)
+        for g, (lo, hi) in enumerate(groups):
+            w = hi - lo
+            nc.vector.tensor_tensor(
+                z_view[:, 2:4, lo:hi],
+                high[0][g][:].rearrange("p (t v) -> p t v", t=2),
+                high[1][g][:].rearrange("p (t v) -> p t v", t=2),
+                MAX,
+            )
+            nc.vector.tensor_copy(
+                z_w[g][:].rearrange("p (c i t) -> p c t i", i=4, t=PACK),
+                z_view[:, :, lo:hi].rearrange("p t (c i) -> p c t i", i=4),
+            )
+            quantize(z_codes[:, lo:hi], z_scales[:, lo:hi], z_w[g][:])
+            second_pass(g, False)
+        for g, (lo, hi) in enumerate(groups):
+            w = hi - lo
+            res = sb("res%d" % g, 2 * w, F32)
             for m in range(2):
-                cols = dst[:, m * width + lo : m * width + lo + PIECE]
-                if m in vector_ms:
-                    nc.vector.tensor_scalar_max(cols, accs[r, m][:], 0.0)
+                if g == len(groups) - 1 and m == 1:
+                    nc.vector.tensor_scalar_max(res[:, m * w : (m + 1) * w], accs[g, m][:], 0.0)
                 else:
-                    nc.scalar.activation(cols, accs[r, m][:], RELU)
-
-        def warm(count):
-            for i in range(count):
-                spare = bank(i, "spare%d" % i, 512)
-                nc.tensor.matmul_mx(
-                    out=spare[:],
-                    lhsT=c_codes[:, 0:P].bitcast(FP8X4),
-                    lhsT_scale=c_scales[:, 0:P],
-                    rhs=x_codes(512, 1024).bitcast(FP8X4),
-                    rhs_scale=x_scales[:, 512:1024],
-                    start=True,
-                    stop=True,
-                )
-
-        def store(src, lo, width):
-            nc.sync.dma_start(out=out_rows[:, :, lo : lo + width], in_=src[:].rearrange("p (m v) -> p m v", m=2))
-
-        def quantize_c(lo, hi, values):
-            quantize(c_codes[:, lo:hi], c_scales[:, lo:hi], values)
-
-        def largest(lo, hi, second):
-            nc.vector.tensor_tensor(region(Z_HIGH, lo, hi), n1_high[:, 2 * lo : 2 * hi], second, MAX)
-
-        def weave_z(lo, hi):
-            weave(z_w[:, PACK * lo : PACK * hi], Z_LOW + 2 * lo, Z_HIGH + 2 * lo, hi - lo)
-
-        quantize_c(0, 256, ca_w[:])
-        for r in range(2):
-            second_pass(r, True, True)
-        warm(2)
-        largest(0, 384, n2_high[:])
-        for t in (2, 3):
-            nc.vector.tensor_copy(slot(region(N2_LAST, 0, PIECE), t - 2), h[t][:].indirect(pos2_sb[:, 24:32]))
-        for t in (2, 3):
-            nc.vector.tensor_copy(slot(region(C_THIRD, 0, PIECE), t - 2), h[t][:].indirect(cen_sb[:, 16:24]))
-        largest(384, V, region(N2_LAST, 0, PIECE))
-        weave_z(0, 256)
-        weave_z(256, 384)
-        weave(cb_w[:], C_LOW + 512, C_THIRD, PIECE)
-        weave_z(384, V)
-        quantize_z(0, 256)
-        for r in range(2):
-            second_pass(r, False, False)
-        quantize_z(256, 384)
-        second_pass(2, False, True)
-        quantize_c(256, 384, cb_w[:])
-        second_pass(2, True, False)
-        for r in range(2):
-            finish(r, res[0], 256, PIECE * r, ())
-        store(res[0], 0, 256)
-        finish(2, res[1], 128, 0, ())
-        store(res[1], PIECE * 2, 128)
-        for t in (2, 3):
-            nc.vector.tensor_copy(c_last.rearrange("p (n t) -> p n t", t=PACK)[:, :, t], h[t][:].indirect(cen_sb[:, 24:32]))
-        quantize_z(384, 512)
-        second_pass(3, False, True)
-        quantize_c(384, V, c_last)
-        second_pass(3, True, False)
-        finish(3, res[2], 128, 0, (1,))
-        store(res[2], PIECE * 3, 128)
+                    nc.scalar.activation(res[:, m * w : (m + 1) * w], accs[g, m][:], RELU)
+            nc.sync.dma_start(out=out_rows[:, :, lo:hi], in_=res[:].rearrange("p (m v) -> p m v", m=2))

from contextlib import ExitStack

import concourse.mybir as mybir

K, T, S, V, H, N = 512, 4096, 1024, 512, 512, 256
FLOPS = 2 * K * H * S + 2 * 2 * H * N * V

F32 = mybir.dt.float32
BF16 = mybir.dt.bfloat16
I32 = mybir.dt.int32
U32 = mybir.dt.uint32
U16 = mybir.dt.uint16
U8 = mybir.dt.uint8
FP8X4 = mybir.dt.float8_e4m3fn_x4
FP4X4 = mybir.dt.float4_e2m1fn_x4
RELU = mybir.ActivationFunctionType.Relu
COPY = mybir.ActivationFunctionType.Copy
MAX = mybir.AluOpType.max
ADD = mybir.AluOpType.add
MULT = mybir.AluOpType.mult

P = 128
PACK = 4
LATE = 384


def tile_picked_sagecat_maxrelu_e_kernel(
    tc, xT, w1, w2_words, w2_scales, w3_words, w3_scales, offs, cen, pos1, pos2, out
):
    nc = tc.nc
    with ExitStack() as ctx:
        keep = ctx.enter_context(tc.tile_pool(name="keep", bufs=1))
        psum = ctx.enter_context(tc.psum_pool(name="psum", bufs=1))

        def sb(name, cols, dtype, tag=None):
            return keep.tile([P, cols], dtype, name=name, tag=tag or name, align_bytes=64)

        def bank(b, name, cols):
            return psum.tile([P, cols], F32, name=name, tag="bank%d" % b)

        def quantize(codes, scales, values):
            nc.vector.quantize_mx(out=codes.bitcast(FP8X4), scales=scales, in_=values)

        offs_sb = keep.tile([P, S // 16], U16, name="offs_sb")
        cen_sb = keep.tile([P, V // 16], U16, name="cen_sb")
        pos1_sb = keep.tile([P, V // 16], U16, name="pos1_sb")
        pos2_sb = keep.tile([P, V // 16], U16, name="pos2_sb")
        x_rows = xT.rearrange("(p j) t -> p j t", j=PACK)
        x_sb = [sb("x%d" % j, T, F32) for j in range(PACK)]
        nc.sync.dma_start(out=x_sb[0][:], in_=x_rows[:, 0, :])
        nc.sync.dma_start(offs_sb[:], offs)
        for j in range(1, PACK):
            nc.sync.dma_start(out=x_sb[j][:], in_=x_rows[:, j, :])
        w1_rows = w1.rearrange("(p j) c -> p j c", j=PACK)
        w1_parts = ((0, 0, H), (2, 0, LATE), (2, LATE, H))
        w1_raw = [sb("w1_raw%d" % u, 2 * (hi - lo), F32) for u, (j, lo, hi) in enumerate(w1_parts)]
        for u, (j, lo, hi) in enumerate(w1_parts):
            nc.sync.dma_start(out=w1_raw[u][:].rearrange("p (j c) -> p j c", j=2), in_=w1_rows[:, j : j + 2, lo:hi])
        nc.sync.dma_start(pos1_sb[:], pos1)
        nc.sync.dma_start(pos2_sb[:], pos2)
        nc.sync.dma_start(cen_sb[:], cen)
        w3_sb = sb("w3_sb", 2 * N, U8)
        w2_sb = sb("w2_sb", 2 * N, U8)
        nc.sync.dma_start(out=w3_sb[:].bitcast(I32), in_=w3_words[0].bitcast(I32))
        nc.sync.dma_start(out=w2_sb[:].bitcast(I32), in_=w2_words[0].bitcast(I32))
        w23_scales = sb("w23_scales", 2 * N, U8)
        nc.vector.memset(w23_scales[:].bitcast(I32), 0)
        for a, rows in enumerate((w3_scales, w2_scales)):
            for q in range(4):
                nc.sync.dma_start(
                    out=w23_scales[32 * q : 32 * q + 4, a * N : (a + 1) * N].bitcast(I32),
                    in_=rows[0, 4 * q : 4 * q + 4, :].bitcast(I32),
                )

        half = S // 2
        xg = [sb("xg%d" % u, PACK * half, BF16) for u in range(2)]
        for j in range(PACK):
            for u in range(2):
                nc.vector.tensor_copy(
                    xg[u][:].rearrange("p (n j) -> p n j", j=PACK)[:, :, j],
                    x_sb[j][:].indirect(offs_sb[:, u * half // 16 : (u + 1) * half // 16]),
                )

        w1_bf = sb("w1_bf", PACK * H, BF16)

        def deal_views(u, ts):
            j, lo, hi = w1_parts[u]
            dealt = w1_bf[:].rearrange("p (t m j) -> p m t j", t=PACK, j=PACK)[:, lo // PACK : hi // PACK, ts, j : j + 2]
            raw = w1_raw[u][:].rearrange("p (j m t) -> p m t j", j=2, t=PACK)[:, :, ts, :]
            return dealt, raw

        nc.scalar.copy(*deal_views(0, 0))
        nc.gpsimd.tensor_scalar(*deal_views(0, slice(1, 4)), 1.0, 0.0, MULT, ADD)
        nc.scalar.copy(*deal_views(1, 0))
        nc.scalar.copy(*deal_views(2, slice(0, 4)))
        nc.scalar.copy(*deal_views(1, slice(1, 4)))

        xa_codes = sb("xa_codes", 256, U32)
        xb_codes = sb("xb_codes", 768, U32, tag="w1_raw2")
        x_scales = sb("x_scales", S, U8)
        w1_codes = sb("w1_codes", H, U32)
        w1_scales = sb("w1_scales", H, U8)

        def quantize_w1(lo, hi):
            quantize(w1_codes[:, lo:hi], w1_scales[:, lo:hi], w1_bf[:, PACK * lo : PACK * hi])

        def x_codes(lo, hi):
            return xa_codes[:, lo:hi] if hi <= 256 else xb_codes[:, lo - 256 : hi - 256]

        def quantize_x(lo, hi):
            quantize(x_codes(lo, hi), x_scales[:, lo:hi], xg[lo // half][:, PACK * (lo % half) : PACK * (lo % half + hi - lo)])

        x_cuts = (0, 256, 512, 768, 896, 1024)
        x_runs = list(zip(x_cuts, x_cuts[1:]))
        quantize_x(0, 256)
        quantize_w1(0, 128)
        for lo, hi in x_runs[1:]:
            quantize_x(lo, hi)
        quantize_w1(128, 256)
        quantize_w1(256, 512)

        h = [sb("h%d" % t, S, F32) for t in range(PACK)]

        def product(acc, t, lo, hi):
            nc.tensor.matmul_mx(
                out=acc,
                lhsT=w1_codes[:, P * t : P * (t + 1)].bitcast(FP8X4),
                lhsT_scale=w1_scales[:, P * t : P * (t + 1)],
                rhs=x_codes(lo, hi).bitcast(FP8X4),
                rhs_scale=x_scales[:, lo:hi],
                start=True,
                stop=True,
            )

        for r, (lo, hi) in enumerate(x_runs):
            acc = bank(r, "acc_h0_%d" % r, hi - lo)
            product(acc[:], 0, lo, hi)
            if r == 3:
                nc.vector.tensor_scalar_max(h[0][:, lo:hi], acc[:], 0.0)
            else:
                nc.scalar.activation(h[0][:, lo:hi], acc[:], RELU)
        for t in range(1, PACK):
            acc = bank((2 * t + 3) % 8, "acc_h%d_0" % t, 512)
            product(acc[:, 0:256], t, 0, 256)
            product(acc[:, 256:512], t, 256, 512)
            nc.scalar.activation(h[t][:, 0:512], acc[:], RELU)
            acc = bank((2 * t + 4) % 8, "acc_h%d_1" % t, 512)
            product(acc[:], t, 512, 1024)
            nc.scalar.activation(h[t][:, 512:1024], acc[:], RELU)

        groups = ((0, 256), (256, 384), (384, 512))
        low = [sb("n%d_low" % d, 2 * V, BF16) for d in range(2)]
        high = [[sb("n%d_high%d" % (d, g), 2 * (hi - lo), BF16) for g, (lo, hi) in enumerate(groups)] for d in range(2)]
        c_pairs = sb("c_pairs", PACK * V, BF16)
        c_w = sb("c_w", PACK * V, BF16)
        z_planes = sb("z_planes", PACK * V, BF16)
        z_w = [sb("z_w%d" % g, PACK * (hi - lo), BF16) for g, (lo, hi) in enumerate(groups)]
        lists = (pos1_sb, pos2_sb)

        for d in range(2):
            nc.vector.tensor_copy(low[d][:, 0:V], h[0][:].indirect(lists[d][:]))
        for t in range(PACK):
            pair = c_pairs[:, 2 * V * (t // 2) : 2 * V * (t // 2 + 1)].rearrange("p (v e) -> p v e", e=2)
            nc.vector.tensor_copy(pair[:, :, t % 2], h[t][:].indirect(cen_sb[:]))
        for d in range(2):
            nc.scalar.activation(low[d][:, V : 2 * V], h[1][:].indirect(lists[d][:]), COPY)
        for g, (lo, hi) in enumerate(groups):
            w = hi - lo
            for t in (2, 3):
                for d in range(2):
                    nc.scalar.activation(
                        high[d][g][:, w * (t - 2) : w * (t - 1)], h[t][:].indirect(lists[d][:, lo // 16 : hi // 16]), COPY
                    )

        c_codes = sb("c_codes", V, U32)
        c_scales = sb("c_scales", V, U8)
        z_codes = sb("z_codes", V, U32)
        z_scales = sb("z_scales", V, U8)
        out_rows = out.rearrange("(m p) v -> p m v", p=P)
        accs = {}

        def second_pass(g, centre):
            lo, hi = groups[g]
            w_sb, a = (w2_sb, 1) if centre else (w3_sb, 0)
            for m in range(2):
                if centre:
                    accs[g, m] = bank((2 * g + m + 2) % 8, "acc_o%d_%d" % (g, m), hi - lo)
                nc.tensor.matmul_mx(
                    out=accs[g, m][:],
                    lhsT=w_sb[:, 2 * P * m : 2 * P * (m + 1)].bitcast(FP4X4),
                    lhsT_scale=w23_scales[:, a * N + P * m : a * N + P * (m + 1)],
                    rhs=(c_codes if centre else z_codes)[:, lo:hi].bitcast(FP8X4),
                    rhs_scale=(c_scales if centre else z_scales)[:, lo:hi],
                    start=centre,
                    stop=not centre,
                )

        nc.vector.tensor_copy(
            c_w[:].bitcast(I32).rearrange("p (c i u) -> p c u i", i=4, u=2),
            c_pairs[:].bitcast(I32).rearrange("p (u c i) -> p c u i", i=4, u=2),
        )
        nc.vector.tensor_tensor(z_planes[:, 0 : 2 * V], low[0][:], low[1][:], MAX)
        quantize(c_codes[:], c_scales[:], c_w[:])
        for g in range(len(groups)):
            second_pass(g, True)
        z_view = z_planes[:].rearrange("p (t v) -> p t v", t=PACK)
        for g, (lo, hi) in enumerate(groups):
            w = hi - lo
            nc.vector.tensor_tensor(
                z_view[:, 2:4, lo:hi],
                high[0][g][:].rearrange("p (t v) -> p t v", t=2),
                high[1][g][:].rearrange("p (t v) -> p t v", t=2),
                MAX,
            )
            nc.vector.tensor_copy(
                z_w[g][:].rearrange("p (c i t) -> p c t i", i=4, t=PACK),
                z_view[:, :, lo:hi].rearrange("p t (c i) -> p c t i", i=4),
            )
            quantize(z_codes[:, lo:hi], z_scales[:, lo:hi], z_w[g][:])
            second_pass(g, False)
        for g, (lo, hi) in enumerate(groups):
            w = hi - lo
            res = sb("res%d" % g, 2 * w, F32)
            for m in range(2):
                if g == len(groups) - 1 and m == 1:
                    nc.vector.tensor_scalar_max(res[:, m * w : (m + 1) * w], accs[g, m][:], 0.0)
                else:
                    nc.scalar.activation(res[:, m * w : (m + 1) * w], accs[g, m][:], RELU)
            nc.sync.dma_start(out=out_rows[:, :, lo:hi], in_=res[:].rearrange("p (m v) -> p m v", m=2))
